import numpy as np, ml_dtypes
CORES = [83,85,87,115,117,119]
N = 6
BF = ml_dtypes.bfloat16
S, A, L, M, R, D = 128, 64, 32, 4, 64, 32
def steps(nx, sy):
    g = np.arange(8); s = np.zeros(8, np.int64); place = np.zeros((N * L, 8), np.int64); cnt = np.zeros((N * L, 8), np.int64)
    for i in range(N * L):
        place[i] = sy[i // L, :, i % L].astype(np.int64) * S + s
        v = nx[i // L, g, place[i]].astype(np.int64)
        s = v % S; cnt[i] = v // S
    return place, cnt
def counts(rng, uneven=False):
    k = np.argsort(rng.random((N, 8, S, A)), -1)
    w = rng.integers(0, 2, k.shape) * M if uneven else rng.integers(0, M + 1, k.shape)
    return np.ascontiguousarray(np.where(k <= M, k, w).transpose(0, 1, 3, 2))
def perms(rng):
    return np.argsort(rng.random((N, 8, A, S)), -1)
def bounds(rng):
    e = np.zeros((8, N + 1), np.int64)
    e[:, 1:N] = np.arange(1, N) * R + rng.integers(-D, D + 1, (8, N - 1)); e[:, N] = N * R - rng.integers(0, D + 1, 8)
    e[0, N] = N * R - D; e[7, N] = N * R
    return e
def draw(rng, to, ct, e, burst=False):
    n = (e[:, 1:] - e[:, :-1])[:, :, None]
    k = (np.arange(L * M) - M * rng.integers(0, L, (8, N, 1))) % (L * M) if burst else np.argsort(rng.random((8, N, L * M)), -1)
    c = np.sum((k < n).reshape(8, N, L, M), axis=-1)
    g = np.arange(8); s = np.zeros(8, np.int64); sy = np.zeros((N, 8, L), np.int32)
    for i in range(N * L):
        q = i // L; ok = ct[q][g, :, s] == c[:, q, i % L][:, None]
        a = np.argmax(np.where(ok, rng.random((8, A)), -1.0), axis=1)
        sy[q, :, i % L] = a; s = to[q][g, a, s]
    return {"nx": (ct * S + to).reshape(N, 8, A * S).astype(np.int32), "em": rng.integers(0, 64 ** M, (N, 8, A * S)).astype(np.int32), "sy": sy}
def setup_inputs(rng):
    to = np.where(rng.random((N, 8, A, 1)) < 0.125, rng.integers(0, S, (N, 8, A, S)), perms(rng))
    return draw(rng, to, counts(rng), bounds(rng))
def setup_inputs_edge(rng):
    e = bounds(rng); g = np.arange(8)[:, None]; r = np.arange(1, N)[None, :]
    e[:, 1:N] = r * R + D * np.where(g % 2 == 0, 1 - 2 * ((r + g // 2) % 2), 1 - 2 * (g // 2 % 2)); e[:, N] = N * R - D * (np.arange(8) // 4)
    return draw(rng, perms(rng), counts(rng), e)
def setup_inputs_even(rng):
    e = bounds(rng); e[:] = np.arange(N + 1) * R
    return draw(rng, perms(rng), counts(rng), e)
def setup_inputs_merge(rng):
    kind = (np.argsort(rng.random((N, 8, A)), -1) % 4)[:, :, :, None]; h = (N, 8, A, 1); s = np.arange(S)
    one = np.where(rng.random(h) < 0.5, rng.integers(0, 2, h) * (S - 1), rng.integers(0, S, h))
    to = np.where(kind == 0, one, np.where(kind == 1, s, np.where(kind == 2, (s + 1) % S, rng.integers(0, S, (N, 8, A, S)))))
    return draw(rng, to, counts(rng), bounds(rng))
def setup_inputs_spread(rng):
    to = np.minimum(np.floor(S * rng.random((N, 8, A, S)) ** 6), S - 1).astype(np.int64)
    d = draw(rng, to, counts(rng, True), bounds(rng), True)
    h = (N, 8, A * S); d["em"] = (d["em"] >> np.where(rng.random(h) < 0.5, rng.integers(0, 6 * M, h), 0)).astype(np.int32)
    return d
def check_inputs(d):
    bad = []
    for k, top in (("nx", (M + 1) * S), ("em", 64 ** M), ("sy", A)):
        if d[k].min() < 0 or d[k].max() >= top: bad.append("range of " + k)
    if bad: return bad
    place, cnt = steps(d["nx"], d["sy"])
    off = np.add.accumulate(cnt, 0)[L - 1::L] - R * np.arange(1, N + 1)[:, None]
    if (np.abs(off) > D).any(): bad.append("running totals")
    if (off[-1] > 0).any(): bad.append("whole total")
    return bad
def reference(nx, em, sy):
    place, cnt = steps(nx, sy); g = np.broadcast_to(np.arange(8), (N * L, 8)); r = (np.arange(N * L) // L)[:, None]
    e = em[r, g, place].astype(np.int64); beg = np.add.accumulate(cnt, 0) - cnt
    z = np.full((8, N * R), -1, np.int64)
    for m in range(M):
        on = cnt > m
        z[g[on], beg[on] + m] = ((e >> (6 * m)) & 63)[on]
    return {"y": np.ascontiguousarray(z.reshape(8, N, R).transpose(1, 0, 2)).astype(np.float32)}

@@ -1,0 +1,438 @@
+from concourse.mybir import dt, AluOpType, AxisListType, ActivationFunctionType
+from concourse.bass import IndirectOffsetOnAxis, DstId, RemoteDMATransfer
+
+SCRATCH = {"emd": ("dram", [512, 128], "int32")}
+for _t, _l in (
+    ("int32", "TN:32,16 TS:32,16 SY:8,16 IDX:2 IDY:2 AE:256 EM:32 E2:2 D:8 P:1 PI:8 DIAG:16"),
+    ("float16", "N16:32,16 OM:256 HF:256 SELH:64 SHMH:128"),
+    ("bfloat16", "TB:16,16 TBLK:32,32 SYM:8,32 OA:128 O:128 XS:32 XR:5,8,4 XQ1:8,16 XQ2:8,16 CF:160 XM:128 "
+                 "CO:256 CZ:256 CO2:256 COC:128 CA:16 CC:16 GTB:64 VB:64 OH0:132 OH1:132 ZB:8 ZP:8 ZN:8 ONES:256 L2:128 "
+                 "SELW:192 BLKA:128 BLK:128 IOTA2:256 SHM:128 NSHM:128 D0:128 TRI:128 IOTAX:132 BC:1 SELC1:64 SELC2:64 "
+                 "SELC:64 SELT:64 CONST:32"),
+    ("uint16", "OFF:256 U0:2 U:160 SA:16 SB:16 REP:4 REP2:8 L16:8"),
+    ("float32", "INJ:4096 WA:256 WB:256 WIN1:128 WIN2:128 SO:256 SOC:128 YS:64 PF:12 PX:1 IO16:16 MASKQ:16 IOR:4 "
+                "IOG:8 II:128 MASKI:128 MT0:32 MT1:32 MT:32 NEG:1 ROUND:1 BI:1"),
+):
+    for _b in _l.split():
+        _n, _d = _b.split(":")
+        SCRATCH[_n] = ("sbuf", [128] + [int(_x) for _x in _d.split(",")], _t)
+for _b in range(8):
+    SCRATCH["B%d" % _b] = ("psum", [128, 512], "float32")
+SEMAPHORES = ["ldsy", "ldn0", "ldn1", "ldn2", "ldn3", "ldem", "ldidx", "v", "t", "s", "gq", "ge",
+              "arr0", "arr1", "arr2", "arr3", "arr4", "arrz", "lsf", "lsz", "st"]
+OP = AluOpType
+FN = ActivationFunctionType
+MOST = 8
+
+
+def common_mask(topo, src, dsts, most):
+    ok = [e for e in topo.engines(src, dsts[0]) if all(e in topo.engines(src, d) for d in dsts)][:most]
+    return sum(1 << e for e in ok), len(ok)
+
+
+def parts(topo, T, r):
+    me, later = T.cores[r], T.cores[r + 1:][::-1]
+    two = ([d for d in later if topo.chip(d) != topo.chip(me)], [d for d in later if topo.chip(d) == topo.chip(me)])
+    return [p for p in two if p]
+
+
+def beside(T, r):
+    return [x for x in (r - 1, r + 1) if 0 <= x < len(T.cores)]
+
+
+def dst_id(topo, d):
+    rid, pid, _ = topo.addr(d)
+    return DstId(rid=rid, pnc=pid)
+
+
+def rank_program(g, core, T, topo):
+    rank = T.rank_of(core)
+    if rank is None:
+        return
+    v, t, s, y = g.vector, g.tensor, g.scalar, g.sync
+    S = T.sem
+    N = len(T.cores)
+    cnt = {"v": 0, "t": 0, "s": 0, "gq": 0}
+    seen = {}
+    queues = {"v": v, "t": t, "s": s, "y": y, "g": g}
+
+    def inc(key, ins):
+        ins.then_inc(S[key], 1)
+        cnt[key] += 1
+        return cnt[key]
+
+    def vi(ins):
+        return inc("v", ins)
+
+    def ti(ins):
+        return inc("t", ins)
+
+    def si(ins):
+        return inc("s", ins)
+
+    def gi(ins):
+        return inc("gq", ins)
+
+    def need(q, key, n):
+        if n and seen.get((q, key), 0) < n:
+            queues[q].wait_ge(S[key], n)
+            seen[(q, key)] = n
+
+    def arrived(q, r):
+        for p in parts(topo, T, r):
+            if core in p:
+                need(q, "arr%d" % r, common_mask(topo, T.cores[r], p, MOST)[1])
+
+    y.dma_start(T.SY[0:1, :, :], T.sy[0::2, :]).then_inc(S.ldsy, 16)
+    s.dma_start(T.SY[1:2, :, :], T.sy[1::2, :]).then_inc(S.ldsy, 16)
+    for i in range(4):
+        (y, s)[i % 2].dma_start(T.TN[:, 8 * i:8 * i + 8, :], T.nx[2 * i:2 * i + 2, :]).then_inc(S["ldn%d" % i], 16)
+    for h in range(2):
+        y.dma_start(T.IDX[:, h:h + 1], T.sy[:, 16 * h:16 * h + 16]).then_inc(S.ldidx, 16)
+    y.wait_ge(S.ldn2, 16)
+    y.dma_start(T.emd[:], T.em[:]).then_inc(S.ldem, 16)
+
+    v_ones = vi(v.memset(T.ONES[:], 1.0))
+    gP = gi(g.iota(T.P[:], [[1, 1]], 0, 1))
+    gIO = gi(g.iota(T.IO16[:], [[1, 16]], 0, 0, allow_small_or_imprecise_dtypes=True))
+    need("g", "v", v_ones)
+    gL2 = gi(g.affine_select(T.L2[0:2, :], T.ONES[0:2, 0:128], [[1, 2], [0, 64]], OP.is_equal, 0.0, 0, -1))
+    gPX = gi(g.iota(T.PX[:], [[1, 1]], 0, 1, allow_small_or_imprecise_dtypes=True))
+    gST = gi(g.affine_select(T.SELT[:], T.ONES[:, 0:64], [[-2000, 2], [-16, 8], [1000, 4]], OP.is_equal, 0.0, -15, 1))
+    vi(v.memset(T.TBLK[:], 0.0))
+    need("v", "gq", gP)
+    vi(v.tensor_scalar(T.PI[:, 0:1], T.P[:], 15, None, OP.bitwise_and))
+    vi(v.tensor_scalar(T.PI[:, 1:2], T.P[:], 4, None, OP.logical_shift_right))
+    vi(v.tensor_scalar(T.PI[:, 2:3], T.P[:], 3, 1, OP.logical_shift_right, OP.bitwise_and))
+    vP = vi(v.tensor_scalar(T.PI[:, 3:4], T.P[:], 63, None, OP.bitwise_and))
+    need("v", "v", vP)
+    vPF = vi(v.tensor_copy(T.PF[:, 0:4], T.PI[:, 0:4]))
+    need("v", "gq", gIO)
+    need("v", "v", vPF)
+    vMQ = vi(v.tensor_scalar(T.MASKQ[:], T.IO16[:], T.PF[:, 0:1], None, OP.is_equal))
+    need("v", "ldsy", 32)
+    vS0 = vi(v.tensor_copy(T.SYM[0:2, :, 0:16], T.SY[0:2, :, :]))
+    vS1 = vi(v.tensor_scalar(T.SYM[0:2, :, 16:32], T.SY[0:2, :, :], 64.0, None, OP.add))
+    need("t", "gq", gL2)
+    need("t", "v", vS0)
+    tSO = ti(t.matmul(T.B3[:, 0:128], T.L2[0:2, :], T.SYM[0:2, :, 0:16], True, True))
+    need("t", "v", vS1)
+    tSY = ti(t.matmul(T.B0[:, 0:256], T.L2[0:2, :], T.SYM[0:2, :, :], True, True))
+    need("s", "t", tSO)
+    need("s", "v", vPF)
+    s1 = si(s.activation(T.OA[:], T.B3[:, 0:128], FN.Abs, bias=T.PF[:, 3:4], scale=-1.0))
+    need("s", "s", s1)
+    sO = si(s.activation(T.O[:], T.OA[:], FN.Relu, bias=1.0, scale=-1.0))
+    vN, blk, vTS = {}, {}, {}
+
+    def rows16(i):
+        r8 = slice(8 * i, 8 * i + 8)
+        need("v", "ldn%d" % i, 16)
+        vN[i] = vi(v.tensor_copy(T.N16[:, r8, :], T.TN[:, r8, :]))
+
+    def states(i):
+        r8 = slice(8 * i, 8 * i + 8)
+        need("v", "ldn%d" % i, 16)
+        vTS[i] = vi(v.tensor_scalar(T.TS[:, r8, :], T.TN[:, r8, :], 127, None, OP.bitwise_and))
+
+    def blocks(i):
+        r8 = slice(8 * i, 8 * i + 8)
+        need("v", "v", vTS[i])
+        if i < 2:
+            n = vi(v.tensor_copy(T.TB[:, r8, :], T.TS[:, r8, :]))
+            need("s", "v", n)
+        for x in range(2):
+            p = slice(64 * x, 64 * x + 64)
+            o = T.TBLK[p, r8, 16 * x:16 * x + 16]
+            if i < 2:
+                blk[i] = ("s", si(s.activation(o, T.TB[p, r8, :], FN.Copy)))
+            else:
+                blk[i] = ("v", vi(v.tensor_copy(o, T.TS[p, r8, :])))
+
+    states(0)
+    rows16(0)
+    blocks(0)
+    need("v", "t", tSY)
+    need("v", "gq", gPX)
+    vOM = vi(v.tensor_scalar(T.OM[:], T.B0[:, 0:256], T.PX[:], None, OP.is_equal))
+    states(1)
+    rows16(1)
+    blocks(1)
+    rows16(2)
+    rows16(3)
+    states(2)
+    states(3)
+    blocks(2)
+    blocks(3)
+    tA = tOFF = 0
+    for kind, i in (("A", 0), ("A", 1), ("A", 2), ("A", 3), ("F", 0), ("F", 1), ("F", 2), ("F", 3)):
+        r8 = slice(8 * i, 8 * i + 8)
+        if kind == "A":
+            need("t", "v", max(vOM, vN[i]))
+            for h in range(2):
+                k = 2 * i + h
+                m = t.matmul(T.B2[32 * i:32 * i + 32, 128 * h:128 * h + 128], T.OM[:, 32 * k:32 * k + 32], T.N16[:, r8, :],
+                             True, True)
+            if i == 3:
+                tA = ti(m)
+        else:
+            need("t", "s", sO)
+            need("t", *blk[i])
+            for c in range(8):
+                m = t.matmul(T.B1[32 * i:32 * i + 32, c:256:8], T.TBLK[:, 8 * i + c, :], T.O[:, 32 * i:32 * i + 32],
+                             True, True)
+            if i == 3:
+                tOFF = ti(m)
+    need("s", "t", tA)
+    need("s", "v", vMQ)
+    sINJ = {}
+    for q in range(15, -1, -1):
+        sINJ[q] = si(s.activation(T.INJ[:, 256 * q:256 * q + 256], T.B2[:, 0:256], FN.Copy, scale=T.MASKQ[:, q:q + 1]))
+    n1 = vi(v.tensor_scalar(T.PF[:, 4:5], T.PF[:, 1:2], 64.0, None, OP.mult))
+    vRD = vi(v.memset(T.ROUND[:], 128.50390625))
+    vNG = vi(v.memset(T.NEG[:], -129.0))
+    need("v", "ldidx", 32)
+    need("v", "v", n1)
+    vID = vi(v.tensor_scalar(T.IDY[:], T.IDX[:], T.PF[:, 4:5], None, OP.add))
+    need("v", "gq", gST)
+    vi(v.tensor_copy(T.SELH[:], T.SELT[:]))
+    need("v", "t", tOFF)
+    last = [vi(v.tensor_copy(T.OFF[:, 128 * h:128 * h + 128], T.B1[:, 128 * h:128 * h + 128])) for h in range(2)]
+    src, base = T.INJ, 15 * 256
+    for n in range(15):
+        q = 14 - n
+        dst = T.HF if n == 14 else (T.WA, T.WB)[n % 2]
+        need("v", "s", sINJ[q])
+        before, W = list(last), src
+        for h in range(2):
+            need("v", "v", last[h])
+            j = 16 * h + q
+            last[h] = vi(v.tensor_tensor(dst[:, 128 * h:128 * h + 128],
+                                         src[:, base + 128 * h:base + 128 * h + 128].indirect(T.OFF[:, 8 * j:8 * j + 8]),
+                                         T.INJ[:, 256 * q + 128 * h:256 * q + 128 * h + 128], OP.add))
+        src, base = dst, 0
+    H = src
+    vH = last
+    n2 = gi(g.affine_select(T.BLKA[:], T.ONES[:, 0:128], [[-16, 8], [0, 16]], OP.is_ge, 0.0, 0, 1))
+    n3 = gi(g.iota(T.MT0[:], [[1, 4], [0, 8]], 0, 0, allow_small_or_imprecise_dtypes=True))
+    n4 = gi(g.affine_select(T.SELW[:], T.ONES[:, 0:192], [[1, 192]], OP.is_equal, 0.0, -32, -1))
+    n6 = gi(g.affine_select(T.SELC1[:], T.ONES[:, 0:64], [[-2000, 2], [-16, 8], [1000, 4]], OP.is_ge, 0.0, -1000, 1))
+    need("g", "gq", n2)
+    n2 = gi(g.affine_select(T.BLK[:], T.BLKA[:], [[16, 8], [0, 16]], OP.is_ge, 0.0, 15, -1))
+    need("g", "gq", n3)
+    n3 = gi(g.affine_select(T.MT1[:], T.MT0[:], [[0, 4], [-16, 8]], OP.is_ge, 100.0, 0, 1))
+    need("g", "gq", n6)
+    n6 = gi(g.affine_select(T.SELC2[:], T.SELC1[:], [[2000, 2], [16, 8], [-1000, 4]], OP.is_ge, 0.0, 1015, -1))
+    gi(g.affine_select(T.D0[:], T.SELW[:, 32:160], [[-16, 8], [0, 16]], OP.is_equal, 0.0, 0, 1))
+    need("g", "gq", n6)
+    gi(g.affine_select(T.SELC[:], T.SELC2[:], [[-2000, 2], [-16, 8], [1000, 4]], OP.not_equal, -128.0, -15, 1))
+    gi(g.affine_select(T.MT[:], T.MT1[:], [[0, 4], [16, 8]], OP.is_ge, 100.0, 15, -1))
+    gi(g.affine_select(T.SHM[:], T.BLK[:], [[1, 128]], OP.is_equal, 0.0, -1, -1))
+    gi(g.iota(T.IOTA2[:], [[0, 2], [1, 128]], 0, 0, allow_small_or_imprecise_dtypes=True))
+    gi(g.iota(T.IOR[:], [[2, 4]], 0, 0, allow_small_or_imprecise_dtypes=True))
+    gi(g.iota(T.IOG[:], [[4, 8]], 0, 0, allow_small_or_imprecise_dtypes=True))
+    gi(g.iota(T.CONST[:], [[0, 16], [-18576, 2]], 16512, 0, allow_small_or_imprecise_dtypes=True))
+    gC = gi(g.iota(T.II[:], [[0, 8], [1, 16]], 0, 0, allow_small_or_imprecise_dtypes=True))
+    need("g", "ldem", 16)
+    need("g", "v", vID)
+    for h in range(2):
+        g.indirect_dma_start(T.AE[:, 128 * h:128 * h + 128], None, T.emd[:],
+                             IndirectOffsetOnAxis(ap=T.IDY[:, h:h + 1], axis=0), bounds_check=511).then_inc(S.ge, 16)
+    need("s", "v", vRD)
+    need("s", "s", sINJ[0])
+    si(s.activation(T.CZ[:], T.INJ[:, 0:256], FN.Identity, bias=T.ROUND[:], scale=1.0 / 128))
+    for h in range(2):
+        need("s", "v", before[h])
+        sCO = si(s.activation(T.CO[:, 128 * h:128 * h + 128], W[:, 128 * h:128 * h + 128].indirect(T.OFF[:, 128 * h:128 * h + 8]),
+                              FN.Identity, bias=T.ROUND[:], scale=1.0 / 128))
+    need("v", "gq", gC)
+    vMI = vi(v.tensor_scalar(T.MASKI[:], T.II[:], T.PF[:, 0:1], None, OP.is_equal))
+    vRP2 = vi(v.tensor_copy(T.REP2[:], T.IOG[:]))
+    need("v", "v", vH[1])
+    vC2 = vi(v.tensor_scalar(T.CO2[:], H[:], 1.0 / 128, 128.50390625, OP.mult, OP.add))
+    o = T.B0[:, 0:32]
+    need("t", "gq", gC)
+    t.matmul(o, T.ONES[0:2, 0:128], T.CONST[0:2, :], True, False)
+    need("t", "s", sCO - 2)
+    for h in range(2):
+        t.matmul(o, T.CZ[:, 128 * h:128 * h + 128], T.SELC[:, 32 * h:32 * h + 32], False, False)
+    need("t", "s", sCO - 1)
+    t.matmul(o, T.CO[:, 0:128], T.SELC[:, 0:32], False, False)
+    need("t", "v", vH[0])
+    t.matmul(o, H[:, 0:128], T.SELH[:, 0:32], False, False)
+    need("t", "s", sCO)
+    t.matmul(o, T.CO[:, 128:256], T.SELC[:, 32:64], False, False)
+    need("t", "v", vH[1])
+    tX = ti(t.matmul(o, H[:, 128:256], T.SELH[:, 32:64], False, True))
+    need("v", "t", tX)
+    vX = vi(v.tensor_copy(T.XS[:], T.B0[:, 0:32]))
+    if rank < N - 1:
+        need("g", "v", vX)
+        nls = 0
+        for part in parts(topo, T, rank):
+            mask, ne = common_mask(topo, core, part, MOST)
+            g.remote_dma_fused([RemoteDMATransfer(dst_ids=[dst_id(topo, d) for d in part], dma_engine_mask=mask,
+                                                  remote_sem=S["arr%d" % rank], srcs=[T.XS[:]],
+                                                  dsts=[T.XR[:, rank, :, :]] * len(part), alu_op=0)],
+                               local_sem=S.lsf)
+            nls += ne
+    gi(g.affine_select(T.TRI[:], T.BLK[:], [[1, 128]], OP.is_gt, 0.0, 0, -1))
+    gALL = gi(g.iota(T.IOTAX[:, 0:131], [[1, 131]], -3, 0, allow_small_or_imprecise_dtypes=True))
+    if rank < N - 1:
+        g.wait_ge(S.lsf, nls)
+    need("v", "v", max(vX, vMI, vRP2))
+    vXM = vi(v.tensor_tensor(T.XM[:], T.XS[:].indirect(T.REP2[:]), T.MASKI[:], OP.mult))
+    vi(v.tensor_copy(T.SHMH[:], T.SHM[:]))
+    vi(v.tensor_scalar(T.NSHM[:], T.SHM[:], -128.0, None, OP.mult))
+    vBI = vi(v.tensor_scalar(T.BI[:], T.PF[:, 0:1], 1.0, 16512.0, OP.min, OP.mult))
+    t.matmul(T.B3[:, 0:256], T.D0[:], T.IOTA2[:], True, False)
+    need("t", "v", vXM)
+    tL = ti(t.matmul(T.B2[:, 0:8], T.XM[:], T.BLK[:, 0::16], True, True))
+    need("t", "v", max(vBI, vC2))
+    t.matmul(T.B3[:, 0:256], T.SHMH[:], H[:], False, False)
+    tS = ti(t.matmul(T.B3[:, 0:256], T.NSHM[:], T.CO2[:], False, True))
+    vi(v.memset(T.BC[:], 2.0 - 4.0 * rank))
+    vi(v.memset(T.U0[:], 0))
+    vXZ = vi(v.tensor_copy(T.DIAG[:], T.MASKQ[:]))
+    if rank:
+        vXZ = vi(v.memset(T.XQ1[:], 0.0))
+    if rank > 4:
+        vXZ = vi(v.memset(T.XQ2[:], 0.0))
+    vRP = vi(v.tensor_scalar(T.REP[:], T.IOR[:], T.PF[:, 2:3], None, OP.add))
+    need("v", "t", tL)
+    vL = vi(v.tensor_copy(T.L16[:], T.B2[:, 0:8]))
+    need("s", "t", tS)
+    need("s", "v", vBI)
+    sSO = si(s.activation(T.SO[:], T.B3[:, 0:256], FN.Identity, bias=T.BI[:]))
+    need("s", "v", vL)
+    sCC = si(s.activation(T.COC[:], T.CO2[:, 128:256].indirect(T.L16[:]), FN.Copy))
+
+    def half1():
+        need("v", "s", sSO)
+        need("v", "v", vL)
+        return vi(v.tensor_copy(T.SOC[:], T.SO[:, 128:256].indirect(T.L16[:])))
+    ucol, L, vU, tail = T.U0[:, 0:1], 0, vRP, []
+    if rank == 0:
+        vSOC = half1()
+    if rank > 0:
+        need("v", "v", vXZ)
+        need("s", "v", vXZ)
+        sQ1 = 0
+        for r in range(min(rank, 4)):
+            if r == 1 and rank > 3:
+                arrived("s", r)
+                sQ1 = si(s.activation(T.XQ1[:, :, 4 * r:4 * r + 4], T.XR[:, r, :, :], FN.Copy))
+            else:
+                arrived("v", r)
+                vQ = vi(v.tensor_copy(T.XQ1[:, :, 4 * r:4 * r + 4], T.XR[:, r, :, :]))
+        vSOC = half1()
+        need("t", "v", vQ)
+        need("t", "s", sQ1)
+        tW = ti(t.matmul(T.B4[:, 0:128], T.XQ1[:, :, :], T.SELW[:, 32:160], True, True))
+        need("v", "t", tW)
+        vi(v.tensor_copy(T.U[:, 0:1], T.B4[:, 0:1]))
+        vW = vi(v.tensor_copy(T.WIN1[:], T.B4[:, 0:128]))
+        sW2 = 0
+        if rank > 4:
+            arrived("s", 4)
+            sQ = si(s.activation(T.XQ2[:, :, 0:4], T.XR[:, 4, :, :], FN.Copy))
+            need("t", "s", sQ)
+            tW2 = ti(t.matmul(T.B5[:, 0:128], T.XQ2[:, :, :], T.SELW[:, 32:160], True, True))
+            need("s", "t", tW2)
+            sW2 = si(s.activation(T.WIN2[:], T.B5[:, 0:128], FN.Copy))
+        need("v", "v", vW)
+        need("s", "v", vW)
+        sC = si(s.activation(T.CF[:, 0:1], T.WIN1[:, 0:1], FN.Copy, scale=T.MASKQ[:, 1:2]))
+        tail.append((T.CF[:, 0:1], sC))
+        ucol = T.U[:, 0:1]
+        for k in range(1, 2 * rank):
+            win = T.WIN1 if k < 8 else T.WIN2
+            row = 2 * (k % 8)
+            if k == 8:
+                need("v", "s", sW2)
+                need("s", "s", sW2)
+            un = T.U[:, 16 * k:16 * k + 16]
+            need("v", "v", vU)
+            need("s", "v", vU)
+            vU = vi(v.tensor_copy(un, win[:, 0:128].indirect(ucol)))
+            sC = si(s.activation(T.CF[:, 16 * k:16 * k + 16], win[:, 0:128].indirect(ucol), FN.Copy,
+                                 scale=T.MASKQ[:, row + 1:row + 2]))
+            tail.append((T.CF[:, 16 * k + L:16 * k + L + 1], sC))
+            ucol, L = T.U[:, 16 * k + L:16 * k + L + 1], row
+    own = slice(L, L + 1)
+    need("s", "v", max(vU, vNG))
+    need("s", "s", sCC)
+    sCA = si(s.activation(T.CA[:], T.CO2[:, 0:128].indirect(ucol), FN.Identity, bias=T.NEG[:]))
+    sCC = si(s.activation(T.CC[:], T.COC[:].indirect(ucol), FN.Identity, bias=T.NEG[:]))
+    need("v", "v", max(vU, vSOC))
+    need("v", "s", sSO)
+    vSA = vi(v.tensor_copy(T.SA[:], T.SO[:, 0:128].indirect(ucol)))
+    vSB = vi(v.tensor_copy(T.SB[:], T.SOC[:].indirect(ucol)))
+    need("t", "v", vXZ)
+    need("t", "gq", gALL)
+    for bank in (T.B6, T.B7):
+        t.matmul(bank[:, 0:1], T.BLK[:], T.BC[:], True, False)
+    for col, sC in tail:
+        need("t", "s", sC)
+        for bank in (T.B6, T.B7):
+            t.matmul(bank[:, 0:1], T.BLK[:], col, False, False)
+    need("t", "s", sCA)
+    tB0 = ti(t.matmul(T.B6[:, 0:1], T.TRI[:], T.CA[:, own], False, True))
+    t.matmul(T.B7[:, 0:1], T.BLK[:], T.CA[:, own], False, False)
+    need("t", "s", sCC)
+    tB1 = ti(t.matmul(T.B7[:, 0:1], T.TRI[:], T.CC[:, own], False, True))
+    v.wait_ge(S.ge, 32)
+    need("v", "v", vSA)
+    vi(v.tensor_tensor(T.EM[:, 0:16], T.AE[:, 0:128].indirect(T.SA[:, own]), T.DIAG[:], OP.mult))
+    need("v", "v", vSB)
+    vE1 = vi(v.tensor_tensor(T.EM[:, 16:32], T.AE[:, 128:256].indirect(T.SB[:, own]), T.DIAG[:], OP.mult))
+    need("v", "s", sCA)
+    vi(v.tensor_scalar(T.GTB[:, 0:32], T.MT[:], T.CA[:, own], None, OP.is_lt))
+    need("v", "v", vE1 - 1)
+    vi(v.tensor_reduce(T.E2[:, 0:1], T.EM[:, 0:16], AxisListType.X, OP.max))
+    need("v", "v", vE1)
+    vR1 = vi(v.tensor_reduce(T.E2[:, 1:2], T.EM[:, 16:32], AxisListType.X, OP.max))
+    need("v", "s", sCC)
+    vG1 = vi(v.tensor_scalar(T.GTB[:, 32:64], T.MT[:], T.CC[:, own], None, OP.is_lt))
+    need("v", "gq", gALL)
+    need("v", "t", tB0)
+    vO0 = vi(v.tensor_scalar(T.OH0[:, 0:131], T.IOTAX[:, 0:131], T.B6[:, 0:1], None, OP.is_equal))
+    need("v", "v", vR1)
+    vi(v.tensor_scalar(T.D[:, 0::4], T.E2[:], 63, None, OP.bitwise_and))
+    for m in range(1, 4):
+        vD = vi(v.tensor_scalar(T.D[:, m::4], T.E2[:], 6 * m, 63, OP.logical_shift_right, OP.bitwise_and))
+    need("v", "t", tB1)
+    vO1 = vi(v.tensor_scalar(T.OH1[:, 0:131], T.IOTAX[:, 0:131], T.B7[:, 0:1], None, OP.is_equal))
+    need("v", "v", vD)
+    vVB = vi(v.tensor_tensor(T.VB[:], T.D[:].indirect(T.REP[:]), T.GTB[:], OP.mult))
+    z = T.B1[:, 0:8]
+    for w, tile in enumerate((T.GTB, T.VB)):
+        for k in range(8):
+            need("t", "v", vVB if w else (vO1 if k > 3 else max(vO0, vG1)))
+            m = k % 4
+            ins = t.matmul(z, (T.OH0, T.OH1)[k // 4][:, 3 - m:131 - m], tile[:, 8 * k:8 * k + 8],
+                           w == 0 and k == 0, w == 1 and k == 7)
+    tZ = ti(ins)
+    need("v", "t", tZ)
+    vZ = vi(v.tensor_copy(T.ZB[:], z))
+    need("g", "v", vZ)
+    near = beside(T, rank)
+    mask, ne = common_mask(topo, core, [T.cores[r] for r in near], MOST)
+    g.remote_dma_fused([RemoteDMATransfer(dst_ids=[dst_id(topo, T.cores[r]) for r in near], dma_engine_mask=mask,
+                                          remote_sem=S.arrz, srcs=[T.ZB[:]],
+                                          dsts=[(T.ZN if r < rank else T.ZP)[:] for r in near], alu_op=0)],
+                       local_sem=S.lsz)
+    g.wait_ge(S.lsz, ne)
+    o = T.B2[0:8, 0:64]
+    need("t", "v", vZ)
+    t.matmul(o, T.ZB[:], T.SELW[:, 64:128], True, False)
+    t.wait_ge(S.arrz, sum(common_mask(topo, T.cores[r], [T.cores[x] for x in beside(T, r)], MOST)[1] for r in near))
+    for n, r in enumerate(near):
+        c = 128 if r < rank else 0
+        ins = t.matmul(o, (T.ZP if r < rank else T.ZN)[:], T.SELW[:, c:c + 64], False, n == len(near) - 1)
+    tY = ti(ins)
+    need("v", "t", tY)
+    vY = vi(v.tensor_scalar(T.YS[0:8, :], o, -1.0, None, OP.add))
+    need("y", "v", vY)
+    y.dma_start(T.y[:], T.YS[0:8, :]).then_inc(S.st, 16)
+    y.wait_ge(S.st, 16)

@@ -1,28 +1,29 @@
 from concourse.mybir import dt, AluOpType, AxisListType, ActivationFunctionType
 from concourse.bass import IndirectOffsetOnAxis, DstId, RemoteDMATransfer
 
-SCRATCH = {"emd": ("dram", [512, 128], "int32")}
+SCRATCH = {"emd": ("dram", [512, 128], "int32"), "nxd": ("dram", [512, 128], "int32")}
 for _t, _l in (
-    ("int32", "TN:32,16 TS:32,16 SY:8,16 IDX:2 IDY:2 AE:256 EM:32 E2:2 D:8 P:1 PI:8 DIAG:16"),
-    ("float16", "N16:32,16 OM:256 HF:256 SELH:64 SHMH:128"),
-    ("bfloat16", "TB:16,16 TBLK:32,32 SYM:8,32 OA:128 O:128 XS:32 XR:5,8,4 XQ1:8,16 XQ2:8,16 CF:160 XM:128 "
-                 "CO:256 CZ:256 CO2:256 COC:128 CA:16 CC:16 GTB:64 VB:64 OH0:132 OH1:132 ZB:8 ZP:8 ZN:8 ONES:256 L2:128 "
-                 "SELW:192 BLKA:128 BLK:128 IOTA2:256 SHM:128 NSHM:128 D0:128 TRI:128 IOTAX:132 BC:1 SELC1:64 SELC2:64 "
-                 "SELC:64 SELT:64 CONST:32"),
-    ("uint16", "OFF:256 U0:2 U:160 SA:16 SB:16 REP:4 REP2:8 L16:8"),
-    ("float32", "INJ:4096 WA:256 WB:256 WIN1:128 WIN2:128 SO:256 SOC:128 YS:64 PF:12 PX:1 IO16:16 MASKQ:16 IOR:4 "
-                "IOG:8 II:128 MASKI:128 MT0:32 MT1:32 MT:32 NEG:1 ROUND:1 BI:1"),
+    ("int32", "TN:32,16 TS:32,16 SY:128 IDX:4 IDY:2 AE:512 EM:32 E2:2 D:8 P:1 PI:8 P16:16 Q16:16"),
+    ("bfloat16", "TB:32,16 TBLK:32,32 SYM:128 O:128 XS:24 XR:96 XQ:128 INJ:2048 W:4096 WS:1536 WIN:128 "
+                 "CM:32 CS:2 CN:4 GTB:64 VBZ:1024 OHM:140 OHZ:200 MS:72 WP:168 WN:72 ONES:128 SC:128 L2:128 "
+                 "ID:128 BLKA:128 BLK:128 TRI:128 BH:128 BL:128 IOTA:128 IOTAM:70 IOTAZ:100 SEL:72 GE:96"),
+    ("uint16", "OFF:256 UR:8 U:288 SZ:18 S0:18 SA:18 REP:4 XL:8 YL:8"),
+    ("float32", "SZF:16 Y1:64 YS:64 PF:12 PX:1 MASKQ:16 DIAGB:16 IOR:4 IOG:8 IO0:8 IO:8 MT0:32 MT1:32 MT:32 "
+                "CNT:1 MR:8 SUM:1"),
 ):
     for _b in _l.split():
         _n, _d = _b.split(":")
         SCRATCH[_n] = ("sbuf", [128] + [int(_x) for _x in _d.split(",")], _t)
 for _b in range(8):
     SCRATCH["B%d" % _b] = ("psum", [128, 512], "float32")
-SEMAPHORES = ["ldsy", "ldn0", "ldn1", "ldn2", "ldn3", "ldem", "ldidx", "v", "t", "s", "gq", "ge",
-              "arr0", "arr1", "arr2", "arr3", "arr4", "arrz", "lsf", "lsz", "st"]
+SEMAPHORES = ["ldsy", "ldn0", "ldn1", "ldn2", "ldn3", "ldem", "ldnx", "ldidx", "v", "t", "s", "gq", "ge",
+              "arr", "u0", "cn", "z0", "z1", "z2", "z3", "z4", "z5", "lsf", "lsz", "st"]
 OP = AluOpType
 FN = ActivationFunctionType
 MOST = 8
+ZS = 5
+BS = 2 * ZS
+S_FIRST, V_FIRST, S_THEN, V_THEN, S_CHAIN, S_LAST = (0, 15), (14, 13), (12, 11), (10, 9), (8, 7, 6, 5, 4, 3), (2, 1)
 
 
 def common_mask(topo, src, dsts, most):
@@ -37,7 +38,7 @@ def parts(topo, T, r):
 
 
 def beside(T, r):
-    return [x for x in (r - 1, r + 1) if 0 <= x < len(T.cores)]
+    return [x for x in (r + 1, r - 1) if 0 <= x < len(T.cores)]
 
 
 def dst_id(topo, d):
@@ -52,7 +53,8 @@ def rank_program(g, core, T, topo):
     v, t, s, y = g.vector, g.tensor, g.scalar, g.sync
     S = T.sem
     N = len(T.cores)
-    cnt = {"v": 0, "t": 0, "s": 0, "gq": 0}
+    sends = rank < N - 1
+    cnt = {"v": 0, "t": 0, "s": 0, "gq": 0, "lsf": 0}
     seen = {}
     queues = {"v": v, "t": t, "s": s, "y": y, "g": g}
 
@@ -78,57 +80,72 @@ def rank_program(g, core, T, topo):
             queues[q].wait_ge(S[key], n)
             seen[(q, key)] = n
 
-    def arrived(q, r):
-        for p in parts(topo, T, r):
-            if core in p:
-                need(q, "arr%d" % r, common_mask(topo, T.cores[r], p, MOST)[1])
+    def send(cores, sem, src, dsts):
+        mask, ne = common_mask(topo, core, cores, MOST)
+        g.remote_dma_fused([RemoteDMATransfer(dst_ids=[dst_id(topo, d) for d in cores], dma_engine_mask=mask,
+                                              remote_sem=S[sem], srcs=[src], dsts=dsts, alu_op=0)], local_sem=S.lsf)
+        cnt["lsf"] += ne
 
-    y.dma_start(T.SY[0:1, :, :], T.sy[0::2, :]).then_inc(S.ldsy, 16)
-    s.dma_start(T.SY[1:2, :, :], T.sy[1::2, :]).then_inc(S.ldsy, 16)
+    def from_parts(ranks):
+        return sum(common_mask(topo, T.cores[r], p, MOST)[1] for r in ranks for p in parts(topo, T, r) if core in p)
+
+    def heard(q, r):
+        need(q, "z%d" % r, common_mask(topo, T.cores[r], [T.cores[x] for x in beside(T, r)], MOST)[1])
+
+    def iota(out, pattern, base, cm=0):
+        return gi(g.iota(out, pattern, base, cm, allow_small_or_imprecise_dtypes=True))
+
+    def blk128(buf, k):
+        return buf[:, 128 * k:128 * k + 128]
+
+    y.dma_start(T.SY[0:1, :], T.sy[0::2, :]).then_inc(S.ldsy, 16)
+    s.dma_start(T.SY[1:2, :], T.sy[1::2, :]).then_inc(S.ldsy, 16)
     for i in range(4):
         (y, s)[i % 2].dma_start(T.TN[:, 8 * i:8 * i + 8, :], T.nx[2 * i:2 * i + 2, :]).then_inc(S["ldn%d" % i], 16)
-    for h in range(2):
-        y.dma_start(T.IDX[:, h:h + 1], T.sy[:, 16 * h:16 * h + 16]).then_inc(S.ldidx, 16)
+    for h, j in enumerate((0, ZS + 1, 16)):
+        y.dma_start(T.IDX[:, h:h + 1], T.sy[:, j:j + 16]).then_inc(S.ldidx, 16)
     y.wait_ge(S.ldn2, 16)
     y.dma_start(T.emd[:], T.em[:]).then_inc(S.ldem, 16)
+    y.dma_start(T.nxd[:], T.nx[:]).then_inc(S.ldnx, 16)
 
+    gP16 = gi(g.iota(T.P16[:], [[-1, 16]], 16, 1))
+    gP = gi(g.iota(T.P[:], [[1, 1]], 0, 4))
+    gI = iota(T.IOTA[:], [[1, 128]], 0)
     v_ones = vi(v.memset(T.ONES[:], 1.0))
-    gP = gi(g.iota(T.P[:], [[1, 1]], 0, 1))
-    gIO = gi(g.iota(T.IO16[:], [[1, 16]], 0, 0, allow_small_or_imprecise_dtypes=True))
     need("g", "v", v_ones)
-    gL2 = gi(g.affine_select(T.L2[0:2, :], T.ONES[0:2, 0:128], [[1, 2], [0, 64]], OP.is_equal, 0.0, 0, -1))
-    gPX = gi(g.iota(T.PX[:], [[1, 1]], 0, 1, allow_small_or_imprecise_dtypes=True))
-    gST = gi(g.affine_select(T.SELT[:], T.ONES[:, 0:64], [[-2000, 2], [-16, 8], [1000, 4]], OP.is_equal, 0.0, -15, 1))
+    gL2 = gi(g.affine_select(T.L2[0:2, :], T.ONES[0:2, :], [[1, 2], [0, 64]], OP.is_equal, 0.0, 0, -1))
     vi(v.memset(T.TBLK[:], 0.0))
     need("v", "gq", gP)
-    vi(v.tensor_scalar(T.PI[:, 0:1], T.P[:], 15, None, OP.bitwise_and))
-    vi(v.tensor_scalar(T.PI[:, 1:2], T.P[:], 4, None, OP.logical_shift_right))
-    vi(v.tensor_scalar(T.PI[:, 2:3], T.P[:], 3, 1, OP.logical_shift_right, OP.bitwise_and))
-    vP = vi(v.tensor_scalar(T.PI[:, 3:4], T.P[:], 63, None, OP.bitwise_and))
-    need("v", "v", vP)
-    vPF = vi(v.tensor_copy(T.PF[:, 0:4], T.PI[:, 0:4]))
-    need("v", "gq", gIO)
-    need("v", "v", vPF)
-    vMQ = vi(v.tensor_scalar(T.MASKQ[:], T.IO16[:], T.PF[:, 0:1], None, OP.is_equal))
+    vi(v.tensor_scalar(T.PI[:, 3:4], T.P[:], 2, 63, OP.logical_shift_right, OP.bitwise_and))
+    n = vi(v.tensor_scalar(T.Q16[:], T.P16[:], 15, None, OP.bitwise_and))
+    vi(v.tensor_scalar(T.PI[:, 0:1], T.P[:], 2, 15, OP.logical_shift_right, OP.bitwise_and))
+    vi(v.tensor_scalar(T.PI[:, 1:2], T.P[:], 448, None, OP.bitwise_and))
+    vP = vi(v.tensor_scalar(T.PI[:, 2:3], T.P[:], 5, 1, OP.logical_shift_right, OP.bitwise_and))
+    need("v", "v", n)
+    vMQ = vi(v.tensor_scalar(T.MASKQ[:], T.Q16[:], 0.0, None, OP.is_equal))
+    vPX = vi(v.tensor_copy(T.PX[:], T.PI[:, 3:4]))
+    inj = {}
+
+    def inj_v(q):
+        need("v", "gq", gI)
+        need("v", "v", vMQ)
+        inj[q] = ("v", vi(v.tensor_scalar(blk128(T.INJ, q), T.IOTA[:], T.MASKQ[:, q:q + 1], None, OP.mult)))
+
+    def inj_s(q):
+        need("s", "gq", gI)
+        need("s", "v", vMQ)
+        inj[q] = ("s", si(s.activation(blk128(T.INJ, q), T.IOTA[:], FN.Copy, scale=T.MASKQ[:, q:q + 1])))
+
+    for q in S_FIRST:
+        inj_s(q)
     need("v", "ldsy", 32)
-    vS0 = vi(v.tensor_copy(T.SYM[0:2, :, 0:16], T.SY[0:2, :, :]))
-    vS1 = vi(v.tensor_scalar(T.SYM[0:2, :, 16:32], T.SY[0:2, :, :], 64.0, None, OP.add))
+    vS0 = vi(v.tensor_copy(T.SYM[0:2, :], T.SY[0:2, :]))
+    for q in V_FIRST:
+        inj_v(q)
     need("t", "gq", gL2)
     need("t", "v", vS0)
-    tSO = ti(t.matmul(T.B3[:, 0:128], T.L2[0:2, :], T.SYM[0:2, :, 0:16], True, True))
-    need("t", "v", vS1)
-    tSY = ti(t.matmul(T.B0[:, 0:256], T.L2[0:2, :], T.SYM[0:2, :, :], True, True))
-    need("s", "t", tSO)
-    need("s", "v", vPF)
-    s1 = si(s.activation(T.OA[:], T.B3[:, 0:128], FN.Abs, bias=T.PF[:, 3:4], scale=-1.0))
-    need("s", "s", s1)
-    sO = si(s.activation(T.O[:], T.OA[:], FN.Relu, bias=1.0, scale=-1.0))
-    vN, blk, vTS = {}, {}, {}
-
-    def rows16(i):
-        r8 = slice(8 * i, 8 * i + 8)
-        need("v", "ldn%d" % i, 16)
-        vN[i] = vi(v.tensor_copy(T.N16[:, r8, :], T.TN[:, r8, :]))
+    tSO = ti(t.matmul(T.B0[:, 0:128], T.L2[0:2, :], T.SYM[0:2, :], True, True))
+    blk, vTS = {}, {}
 
     def states(i):
         r8 = slice(8 * i, 8 * i + 8)
@@ -138,301 +155,280 @@ def rank_program(g, core, T, topo):
     def blocks(i):
         r8 = slice(8 * i, 8 * i + 8)
         need("v", "v", vTS[i])
-        if i < 2:
-            n = vi(v.tensor_copy(T.TB[:, r8, :], T.TS[:, r8, :]))
-            need("s", "v", n)
-        for x in range(2):
-            p = slice(64 * x, 64 * x + 64)
-            o = T.TBLK[p, r8, 16 * x:16 * x + 16]
-            if i < 2:
-                blk[i] = ("s", si(s.activation(o, T.TB[p, r8, :], FN.Copy)))
-            else:
-                blk[i] = ("v", vi(v.tensor_copy(o, T.TS[p, r8, :])))
+        need("s", "v", vTS[i])
+        blk[i] = (vi(v.tensor_copy(T.TBLK[0:64, r8, 0:16], T.TS[0:64, r8, :])),
+                  si(s.activation(T.TBLK[64:128, r8, 16:32], T.TS[64:128, r8, :], FN.Copy)))
 
     states(0)
-    rows16(0)
-    blocks(0)
-    need("v", "t", tSY)
-    need("v", "gq", gPX)
-    vOM = vi(v.tensor_scalar(T.OM[:], T.B0[:, 0:256], T.PX[:], None, OP.is_equal))
     states(1)
-    rows16(1)
-    blocks(1)
-    rows16(2)
-    rows16(3)
+    blocks(0)
+    need("v", "t", tSO)
+    need("v", "v", vPX)
+    vO = vi(v.tensor_scalar(T.O[:], T.B0[:, 0:128], T.PX[:], None, OP.is_equal))
     states(2)
+    blocks(1)
     states(3)
     blocks(2)
     blocks(3)
-    tA = tOFF = 0
-    for kind, i in (("A", 0), ("A", 1), ("A", 2), ("A", 3), ("F", 0), ("F", 1), ("F", 2), ("F", 3)):
-        r8 = slice(8 * i, 8 * i + 8)
-        if kind == "A":
-            need("t", "v", max(vOM, vN[i]))
-            for h in range(2):
-                k = 2 * i + h
-                m = t.matmul(T.B2[32 * i:32 * i + 32, 128 * h:128 * h + 128], T.OM[:, 32 * k:32 * k + 32], T.N16[:, r8, :],
-                             True, True)
-            if i == 3:
-                tA = ti(m)
-        else:
-            need("t", "s", sO)
-            need("t", *blk[i])
-            for c in range(8):
-                m = t.matmul(T.B1[32 * i:32 * i + 32, c:256:8], T.TBLK[:, 8 * i + c, :], T.O[:, 32 * i:32 * i + 32],
-                             True, True)
-            if i == 3:
-                tOFF = ti(m)
-    need("s", "t", tA)
-    need("s", "v", vMQ)
-    sINJ = {}
-    for q in range(15, -1, -1):
-        sINJ[q] = si(s.activation(T.INJ[:, 256 * q:256 * q + 256], T.B2[:, 0:256], FN.Copy, scale=T.MASKQ[:, q:q + 1]))
-    n1 = vi(v.tensor_scalar(T.PF[:, 4:5], T.PF[:, 1:2], 64.0, None, OP.mult))
-    vRD = vi(v.memset(T.ROUND[:], 128.50390625))
-    vNG = vi(v.memset(T.NEG[:], -129.0))
-    need("v", "ldidx", 32)
+    for i in range(4):
+        need("t", "v", max(vO, blk[i][0]))
+        need("t", "s", blk[i][1])
+        for c in range(8):
+            m = t.matmul(T.B1[32 * i:32 * i + 32, c:256:8], T.TBLK[:, 8 * i + c, :], T.O[:, 32 * i:32 * i + 32], True, True)
+    tOFF = ti(m)
+    for q in S_THEN:
+        inj_s(q)
+    vi(v.tensor_copy(T.PF[:, 0:3], T.PI[:, 0:3]))
+    vi(v.tensor_scalar(T.PF[:, 5:6], T.PI[:, 0:1], ZS + 0.5, None, OP.is_lt))
+    vi(v.tensor_scalar(T.PF[:, 6:7], T.PI[:, 0:1], ZS + 0.5, None, OP.is_gt))
+    n1 = vi(v.tensor_scalar(T.PI[:, 4:5], T.PI[:, 0:1], -1.0, 1.0 / 3, OP.add, OP.mult))
+    inj_v(V_THEN[0])
+    need("v", "ldidx", 48)
     need("v", "v", n1)
-    vID = vi(v.tensor_scalar(T.IDY[:], T.IDX[:], T.PF[:, 4:5], None, OP.add))
-    need("v", "gq", gST)
-    vi(v.tensor_copy(T.SELH[:], T.SELT[:]))
+    n1 = vi(v.tensor_scalar(T.PF[:, 7:8], T.IDX[:, 2:3], T.PF[:, 6:7], T.PF[:, 1:2], OP.mult, OP.add))
+    vi(v.tensor_scalar(T.IDY[:, 1:2], T.IDX[:, 1:2], T.PF[:, 1:2], None, OP.add))
+    vQ3 = vi(v.tensor_scalar(T.PF[:, 8:9], T.PI[:, 4:5], 21.0, T.PF[:, 0:1], OP.mult, OP.add))
+    for q in V_THEN[1:]:
+        inj_v(q)
     need("v", "t", tOFF)
-    last = [vi(v.tensor_copy(T.OFF[:, 128 * h:128 * h + 128], T.B1[:, 128 * h:128 * h + 128])) for h in range(2)]
-    src, base = T.INJ, 15 * 256
-    for n in range(15):
-        q = 14 - n
-        dst = T.HF if n == 14 else (T.WA, T.WB)[n % 2]
-        need("v", "s", sINJ[q])
-        before, W = list(last), src
-        for h in range(2):
-            need("v", "v", last[h])
-            j = 16 * h + q
-            last[h] = vi(v.tensor_tensor(dst[:, 128 * h:128 * h + 128],
-                                         src[:, base + 128 * h:base + 128 * h + 128].indirect(T.OFF[:, 8 * j:8 * j + 8]),
-                                         T.INJ[:, 256 * q + 128 * h:256 * q + 128 * h + 128], OP.add))
-        src, base = dst, 0
-    H = src
-    vH = last
-    n2 = gi(g.affine_select(T.BLKA[:], T.ONES[:, 0:128], [[-16, 8], [0, 16]], OP.is_ge, 0.0, 0, 1))
-    n3 = gi(g.iota(T.MT0[:], [[1, 4], [0, 8]], 0, 0, allow_small_or_imprecise_dtypes=True))
-    n4 = gi(g.affine_select(T.SELW[:], T.ONES[:, 0:192], [[1, 192]], OP.is_equal, 0.0, -32, -1))
-    n6 = gi(g.affine_select(T.SELC1[:], T.ONES[:, 0:64], [[-2000, 2], [-16, 8], [1000, 4]], OP.is_ge, 0.0, -1000, 1))
+    vOA = vi(v.tensor_copy(T.OFF[:, 8 * BS:256], T.B1[:, 8 * BS:256]))
+    vOB = vi(v.tensor_copy(T.OFF[:, 0:8 * BS], T.B1[:, 0:8 * BS]))
+    need("v", "v", n1)
+    vID = vi(v.tensor_scalar(T.IDY[:, 0:1], T.IDX[:, 0:1], T.PF[:, 5:6], T.PF[:, 7:8], OP.mult, OP.add))
+    sB = 0
+    rows = list(S_CHAIN)
+    if sends:
+        need("s", "v", vOB)
+        for j in range(BS - 1, -1, -1):
+            need("s", "s", sB)
+            win = T.IOTA[:] if j == BS - 1 else blk128(T.WS, j + 1)
+            sB = si(s.activation(blk128(T.WS, j), win.indirect(T.OFF[:, 8 * j:8 * j + 8]), FN.Copy))
+            if rows and j:
+                inj_s(rows.pop(0))
+    for q in rows + list(S_LAST):
+        inj_s(q)
+
+    def row(j):
+        return j + 1 if j < ZS else j - ZS if j < ZS + 16 else (j - 15) % 16
+
+    done = {}
+
+    def step(j):
+        first = j in (31, ZS + 15, ZS - 1)
+        win = blk128(T.INJ, row(j)) if first else blk128(T.W, j + 1)
+        need("v", *(inj[row(j)] if first else ("v", done[j + 1])))
+        need("v", "v", vOA if j >= BS else vOB)
+        a = win.indirect(T.OFF[:, 8 * j:8 * j + 8])
+        if j in (ZS, ZS + 16):
+            done[j] = vi(v.tensor_copy(blk128(T.W, j), a))
+        else:
+            need("v", *inj[row(j - 1)])
+            done[j] = vi(v.tensor_tensor(blk128(T.W, j), a, blk128(T.INJ, row(j - 1)), OP.add))
+
+    for n in range(16 - ZS):
+        if rank == 0 and n == 15 - ZS:
+            need("v", "s", sB)
+            vi(v.memset(T.U[:, 53:54], 0))
+            vU = vi(v.tensor_copy(T.U[:, 0:1], T.WS[:, 0:1]))
+        step(ZS + 15 - n)
+        step(31 - n)
+    later = [j for n in range(ZS) for j in (ZS - 1 - n, BS - 1 - n)]
+    gi(g.affine_select(T.SEL[:, 0:48], T.ONES[:, 0:48], [[-2000, 2], [-16, 8], [1000, 3]], OP.is_equal, 0.0, 0, 1))
+    gi(g.affine_select(T.SEL[:, 48:72], T.ONES[:, 0:24], [[-16, 8], [1000, 3]], OP.is_equal, 0.0, -1015, 1))
+    n2 = gi(g.affine_select(T.SC[:], T.ONES[:], [[0, 128]], OP.is_gt, 1.0 / 128, 0, 0))
+    n3 = iota(T.MT0[:], [[128, 4], [0, 8]], 128 * 129)
+    need("g", "gq", n2)
+    n2 = gi(g.affine_select(T.BLKA[:], T.SC[:], [[-16, 8], [0, 16]], OP.is_ge, 0.0, 0, 1))
+    gi(g.affine_select(T.ID[:], T.ONES[:], [[1, 128]], OP.is_equal, 0.0, 0, -1))
     need("g", "gq", n2)
     n2 = gi(g.affine_select(T.BLK[:], T.BLKA[:], [[16, 8], [0, 16]], OP.is_ge, 0.0, 15, -1))
+    n3 = gi(g.affine_select(T.MT1[:], T.MT0[:], [[0, 4], [-16, 8]], OP.is_ge, 1e6, 0, 1))
+    iota(T.IOR[:], [[2, 4]], 0)
+    iota(T.IOG[:], [[3, 8]], 0)
     need("g", "gq", n3)
-    n3 = gi(g.affine_select(T.MT1[:], T.MT0[:], [[0, 4], [-16, 8]], OP.is_ge, 100.0, 0, 1))
-    need("g", "gq", n6)
-    n6 = gi(g.affine_select(T.SELC2[:], T.SELC1[:], [[2000, 2], [16, 8], [-1000, 4]], OP.is_ge, 0.0, 1015, -1))
-    gi(g.affine_select(T.D0[:], T.SELW[:, 32:160], [[-16, 8], [0, 16]], OP.is_equal, 0.0, 0, 1))
-    need("g", "gq", n6)
-    gi(g.affine_select(T.SELC[:], T.SELC2[:], [[-2000, 2], [-16, 8], [1000, 4]], OP.not_equal, -128.0, -15, 1))
-    gi(g.affine_select(T.MT[:], T.MT1[:], [[0, 4], [16, 8]], OP.is_ge, 100.0, 15, -1))
-    gi(g.affine_select(T.SHM[:], T.BLK[:], [[1, 128]], OP.is_equal, 0.0, -1, -1))
-    gi(g.iota(T.IOTA2[:], [[0, 2], [1, 128]], 0, 0, allow_small_or_imprecise_dtypes=True))
-    gi(g.iota(T.IOR[:], [[2, 4]], 0, 0, allow_small_or_imprecise_dtypes=True))
-    gi(g.iota(T.IOG[:], [[4, 8]], 0, 0, allow_small_or_imprecise_dtypes=True))
-    gi(g.iota(T.CONST[:], [[0, 16], [-18576, 2]], 16512, 0, allow_small_or_imprecise_dtypes=True))
-    gC = gi(g.iota(T.II[:], [[0, 8], [1, 16]], 0, 0, allow_small_or_imprecise_dtypes=True))
-    need("g", "ldem", 16)
-    need("g", "v", vID)
-    for h in range(2):
-        g.indirect_dma_start(T.AE[:, 128 * h:128 * h + 128], None, T.emd[:],
-                             IndirectOffsetOnAxis(ap=T.IDY[:, h:h + 1], axis=0), bounds_check=511).then_inc(S.ge, 16)
-    need("s", "v", vRD)
-    need("s", "s", sINJ[0])
-    si(s.activation(T.CZ[:], T.INJ[:, 0:256], FN.Identity, bias=T.ROUND[:], scale=1.0 / 128))
-    for h in range(2):
-        need("s", "v", before[h])
-        sCO = si(s.activation(T.CO[:, 128 * h:128 * h + 128], W[:, 128 * h:128 * h + 128].indirect(T.OFF[:, 128 * h:128 * h + 8]),
-                              FN.Identity, bias=T.ROUND[:], scale=1.0 / 128))
-    need("v", "gq", gC)
-    vMI = vi(v.tensor_scalar(T.MASKI[:], T.II[:], T.PF[:, 0:1], None, OP.is_equal))
-    vRP2 = vi(v.tensor_copy(T.REP2[:], T.IOG[:]))
-    need("v", "v", vH[1])
-    vC2 = vi(v.tensor_scalar(T.CO2[:], H[:], 1.0 / 128, 128.50390625, OP.mult, OP.add))
-    o = T.B0[:, 0:32]
-    need("t", "gq", gC)
-    t.matmul(o, T.ONES[0:2, 0:128], T.CONST[0:2, :], True, False)
-    need("t", "s", sCO - 2)
-    for h in range(2):
-        t.matmul(o, T.CZ[:, 128 * h:128 * h + 128], T.SELC[:, 32 * h:32 * h + 32], False, False)
-    need("t", "s", sCO - 1)
-    t.matmul(o, T.CO[:, 0:128], T.SELC[:, 0:32], False, False)
-    need("t", "v", vH[0])
-    t.matmul(o, H[:, 0:128], T.SELH[:, 0:32], False, False)
-    need("t", "s", sCO)
-    t.matmul(o, T.CO[:, 128:256], T.SELC[:, 32:64], False, False)
-    need("t", "v", vH[1])
-    tX = ti(t.matmul(o, H[:, 128:256], T.SELH[:, 32:64], False, True))
-    need("v", "t", tX)
-    vX = vi(v.tensor_copy(T.XS[:], T.B0[:, 0:32]))
-    if rank < N - 1:
-        need("g", "v", vX)
-        nls = 0
-        for part in parts(topo, T, rank):
-            mask, ne = common_mask(topo, core, part, MOST)
-            g.remote_dma_fused([RemoteDMATransfer(dst_ids=[dst_id(topo, d) for d in part], dma_engine_mask=mask,
-                                                  remote_sem=S["arr%d" % rank], srcs=[T.XS[:]],
-                                                  dsts=[T.XR[:, rank, :, :]] * len(part), alu_op=0)],
-                               local_sem=S.lsf)
-            nls += ne
+    gi(g.affine_select(T.MT[:], T.MT1[:], [[0, 4], [16, 8]], OP.is_ge, 1e6, 15, -1))
     gi(g.affine_select(T.TRI[:], T.BLK[:], [[1, 128]], OP.is_gt, 0.0, 0, -1))
-    gALL = gi(g.iota(T.IOTAX[:, 0:131], [[1, 131]], -3, 0, allow_small_or_imprecise_dtypes=True))
-    if rank < N - 1:
-        g.wait_ge(S.lsf, nls)
-    need("v", "v", max(vX, vMI, vRP2))
-    vXM = vi(v.tensor_tensor(T.XM[:], T.XS[:].indirect(T.REP2[:]), T.MASKI[:], OP.mult))
-    vi(v.tensor_copy(T.SHMH[:], T.SHM[:]))
-    vi(v.tensor_scalar(T.NSHM[:], T.SHM[:], -128.0, None, OP.mult))
-    vBI = vi(v.tensor_scalar(T.BI[:], T.PF[:, 0:1], 1.0, 16512.0, OP.min, OP.mult))
-    t.matmul(T.B3[:, 0:256], T.D0[:], T.IOTA2[:], True, False)
-    need("t", "v", vXM)
-    tL = ti(t.matmul(T.B2[:, 0:8], T.XM[:], T.BLK[:, 0::16], True, True))
-    need("t", "v", max(vBI, vC2))
-    t.matmul(T.B3[:, 0:256], T.SHMH[:], H[:], False, False)
-    tS = ti(t.matmul(T.B3[:, 0:256], T.NSHM[:], T.CO2[:], False, True))
-    vi(v.memset(T.BC[:], 2.0 - 4.0 * rank))
-    vi(v.memset(T.U0[:], 0))
-    vXZ = vi(v.tensor_copy(T.DIAG[:], T.MASKQ[:]))
-    if rank:
-        vXZ = vi(v.memset(T.XQ1[:], 0.0))
-    if rank > 4:
-        vXZ = vi(v.memset(T.XQ2[:], 0.0))
-    vRP = vi(v.tensor_scalar(T.REP[:], T.IOR[:], T.PF[:, 2:3], None, OP.add))
-    need("v", "t", tL)
-    vL = vi(v.tensor_copy(T.L16[:], T.B2[:, 0:8]))
-    need("s", "t", tS)
-    need("s", "v", vBI)
-    sSO = si(s.activation(T.SO[:], T.B3[:, 0:256], FN.Identity, bias=T.BI[:]))
-    need("s", "v", vL)
-    sCC = si(s.activation(T.COC[:], T.CO2[:, 128:256].indirect(T.L16[:]), FN.Copy))
+    gC = iota(T.IO0[:], [[-67, 2], [16, 4]], 64 * rank + 72)
+    need("g", "v", vID)
 
-    def half1():
-        need("v", "s", sSO)
-        need("v", "v", vL)
-        return vi(v.tensor_copy(T.SOC[:], T.SO[:, 128:256].indirect(T.L16[:])))
-    ucol, L, vU, tail = T.U0[:, 0:1], 0, vRP, []
+    def fetch(w):
+        need("g", ("ldem", "ldnx")[w], 16)
+        for h in range(2):
+            g.indirect_dma_start(blk128(T.AE, 2 * h + w), None, (T.emd, T.nxd)[w][:],
+                                 IndirectOffsetOnAxis(ap=T.IDY[:, h:h + 1], axis=0), bounds_check=511).then_inc(S.ge, 16)
+
+    fetch(0)
+    need("t", "gq", gC)
     if rank == 0:
-        vSOC = half1()
-    if rank > 0:
-        need("v", "v", vXZ)
-        need("s", "v", vXZ)
-        sQ1 = 0
-        for r in range(min(rank, 4)):
-            if r == 1 and rank > 3:
-                arrived("s", r)
-                sQ1 = si(s.activation(T.XQ1[:, :, 4 * r:4 * r + 4], T.XR[:, r, :, :], FN.Copy))
-            else:
-                arrived("v", r)
-                vQ = vi(v.tensor_copy(T.XQ1[:, :, 4 * r:4 * r + 4], T.XR[:, r, :, :]))
-        vSOC = half1()
+        need("v", "v", done[BS])
+        n = vi(v.tensor_copy(T.U[:, 18:34], blk128(T.W, BS).indirect(T.U[:, 0:1])))
+        step(later.pop(0))
+        need("v", "v", n)
+        n = vi(v.tensor_copy(T.U[:, 37:53], blk128(T.W, ZS + 16).indirect(T.U[:, 18:19])))
+        need("g", "v", n)
+        for part in parts(topo, T, rank):
+            send(part, "u0", T.U[:, 52:54], [T.UR[:, 0:2]] * len(part))
+    elif sends:
+        o = T.B2[:, 0:24]
+        need("t", "v", done[BS])
+        t.matmul(o, blk128(T.W, BS), T.SEL[:, 48:72], True, False)
+        need("t", "s", sB)
+        t.matmul(o, blk128(T.WS, 0), T.SEL[:, 0:24], False, False)
+        need("t", "v", done[ZS + 16])
+        tX = ti(t.matmul(o, blk128(T.W, ZS + 16), T.SEL[:, 24:48], False, True))
+        step(later.pop(0))
+        step(later.pop(0))
+        need("v", "t", tX)
+        vX = vi(v.tensor_copy(T.XS[:], o))
+        need("g", "v", vX)
+        for part in parts(topo, T, rank):
+            send(part, "arr", T.XS[:], [T.XR[:, 24 * rank - 24:24 * rank]] * len(part))
+    fetch(1)
+    gi(g.affine_select(T.BH[:], T.BLK[:], [[0, 8], [1, 16]], OP.is_ge, 0.0, -ZS - 1, 0))
+    gi(g.affine_select(T.BL[:], T.BLK[:], [[16, 8], [0, 16]], OP.is_ge, 0.0, ZS, -1))
+    iota(T.CN[:], [[16512, 2], [0, 2]], -16512)
+    iota(T.IOTAM[:], [[-32, 2], [1, 35]], -3)
+    iota(T.IOTAZ[:], [[1, 100]], -3)
+    iota(T.MS[:, 0:5], [[0, 5]], 0)
+    if rank == 0:
+        iota(T.WP[:, 0:72], [[0, 72]], 0)
+    gALL = cnt["gq"]
+    for j in later:
+        step(j)
+    sDB = si(s.activation(T.DIAGB[:], T.MASKQ[:], FN.Copy, scale=16448.5))
+    need("s", "s", inj[1][1])
+    sVZ = si(s.activation(T.VBZ[:], T.INJ[:, 0:1024], FN.Copy, scale=0.0))
+    need("s", "gq", gC)
+    need("s", "v", vOB)
+    sIO = si(s.activation(T.IO[:], T.IO0[:], FN.Identity, bias=T.PF[:, 0:1]))
+    need("v", "gq", gC)
+    vRP = vi(v.tensor_scalar(T.REP[:], T.IOR[:], T.PF[:, 2:3], None, OP.add))
+    ucol, L, vU = T.UR[:, 0:1], 0, 0
+    if rank == 0:
+        vU = vi(v.memset(T.UR[:], 0))
+    if rank > 1:
+        wide = 24 * (rank - 1)
+        vXL = vi(v.tensor_scalar(T.XL[:], T.IOG[:], T.PF[:, 8:9], wide - 1.0, OP.add, OP.min))
+        for q in "vs":
+            need(q, "v", vXL)
+            need(q, "arr", from_parts(range(1, rank)))
+        vQ = vi(v.tensor_copy(T.XQ[:, 0:64], T.XR[:, 0:wide].indirect(T.XL[:, 0:4])))
+        sQ = si(s.activation(T.XQ[:, 64:128], T.XR[:, 0:wide].indirect(T.XL[:, 4:8]), FN.Copy))
         need("t", "v", vQ)
-        need("t", "s", sQ1)
-        tW = ti(t.matmul(T.B4[:, 0:128], T.XQ1[:, :, :], T.SELW[:, 32:160], True, True))
+        need("t", "s", sQ)
+        tW = ti(t.matmul(T.B4[:, 0:128], T.XQ[:], T.ID[:], True, True))
         need("v", "t", tW)
-        vi(v.tensor_copy(T.U[:, 0:1], T.B4[:, 0:1]))
-        vW = vi(v.tensor_copy(T.WIN1[:], T.B4[:, 0:128]))
-        sW2 = 0
-        if rank > 4:
-            arrived("s", 4)
-            sQ = si(s.activation(T.XQ2[:, :, 0:4], T.XR[:, 4, :, :], FN.Copy))
-            need("t", "s", sQ)
-            tW2 = ti(t.matmul(T.B5[:, 0:128], T.XQ2[:, :, :], T.SELW[:, 32:160], True, True))
-            need("s", "t", tW2)
-            sW2 = si(s.activation(T.WIN2[:], T.B5[:, 0:128], FN.Copy))
-        need("v", "v", vW)
-        need("s", "v", vW)
-        sC = si(s.activation(T.CF[:, 0:1], T.WIN1[:, 0:1], FN.Copy, scale=T.MASKQ[:, 1:2]))
-        tail.append((T.CF[:, 0:1], sC))
-        ucol = T.U[:, 0:1]
-        for k in range(1, 2 * rank):
-            win = T.WIN1 if k < 8 else T.WIN2
-            row = 2 * (k % 8)
-            if k == 8:
-                need("v", "s", sW2)
-                need("s", "s", sW2)
-            un = T.U[:, 16 * k:16 * k + 16]
-            need("v", "v", vU)
-            need("s", "v", vU)
-            vU = vi(v.tensor_copy(un, win[:, 0:128].indirect(ucol)))
-            sC = si(s.activation(T.CF[:, 16 * k:16 * k + 16], win[:, 0:128].indirect(ucol), FN.Copy,
-                                 scale=T.MASKQ[:, row + 1:row + 2]))
-            tail.append((T.CF[:, 16 * k + L:16 * k + L + 1], sC))
-            ucol, L = T.U[:, 16 * k + L:16 * k + L + 1], row
-    own = slice(L, L + 1)
-    need("s", "v", max(vU, vNG))
-    need("s", "s", sCC)
-    sCA = si(s.activation(T.CA[:], T.CO2[:, 0:128].indirect(ucol), FN.Identity, bias=T.NEG[:]))
-    sCC = si(s.activation(T.CC[:], T.COC[:].indirect(ucol), FN.Identity, bias=T.NEG[:]))
-    need("v", "v", max(vU, vSOC))
-    need("v", "s", sSO)
-    vSA = vi(v.tensor_copy(T.SA[:], T.SO[:, 0:128].indirect(ucol)))
-    vSB = vi(v.tensor_copy(T.SB[:], T.SOC[:].indirect(ucol)))
-    need("t", "v", vXZ)
+        vU = vi(v.tensor_copy(T.WIN[:], T.B4[:, 0:128]))
     need("t", "gq", gALL)
-    for bank in (T.B6, T.B7):
-        t.matmul(bank[:, 0:1], T.BLK[:], T.BC[:], True, False)
-    for col, sC in tail:
-        need("t", "s", sC)
-        for bank in (T.B6, T.B7):
-            t.matmul(bank[:, 0:1], T.BLK[:], col, False, False)
-    need("t", "s", sCA)
-    tB0 = ti(t.matmul(T.B6[:, 0:1], T.TRI[:], T.CA[:, own], False, True))
-    t.matmul(T.B7[:, 0:1], T.BLK[:], T.CA[:, own], False, False)
-    need("t", "s", sCC)
-    tB1 = ti(t.matmul(T.B7[:, 0:1], T.TRI[:], T.CC[:, own], False, True))
-    v.wait_ge(S.ge, 32)
-    need("v", "v", vSA)
-    vi(v.tensor_tensor(T.EM[:, 0:16], T.AE[:, 0:128].indirect(T.SA[:, own]), T.DIAG[:], OP.mult))
-    need("v", "v", vSB)
-    vE1 = vi(v.tensor_tensor(T.EM[:, 16:32], T.AE[:, 128:256].indirect(T.SB[:, own]), T.DIAG[:], OP.mult))
-    need("v", "s", sCA)
-    vi(v.tensor_scalar(T.GTB[:, 0:32], T.MT[:], T.CA[:, own], None, OP.is_lt))
-    need("v", "v", vE1 - 1)
-    vi(v.tensor_reduce(T.E2[:, 0:1], T.EM[:, 0:16], AxisListType.X, OP.max))
-    need("v", "v", vE1)
-    vR1 = vi(v.tensor_reduce(T.E2[:, 1:2], T.EM[:, 16:32], AxisListType.X, OP.max))
-    need("v", "s", sCC)
-    vG1 = vi(v.tensor_scalar(T.GTB[:, 32:64], T.MT[:], T.CC[:, own], None, OP.is_lt))
-    need("v", "gq", gALL)
-    need("v", "t", tB0)
-    vO0 = vi(v.tensor_scalar(T.OH0[:, 0:131], T.IOTAX[:, 0:131], T.B6[:, 0:1], None, OP.is_equal))
-    need("v", "v", vR1)
+    t.matmul(T.B6[:, 0:3], T.TRI[:], T.CN[:, 0:3], True, False)
+    for col, mat in ((0, T.BH), (1, T.BL), (2, T.BLK), (2, T.BLK)):
+        t.matmul(T.B6[:, col:col + 1], mat[:], T.CN[:, 0:1], False, False)
+    if rank:
+        need("v", "u0", from_parts([0]))
+        need("s", "u0", from_parts([0]))
+    for k in range(3 * rank - 3):
+        a = 18 * k + L % 2
+        need("v", "v", vU)
+        vU = vi(v.tensor_copy(T.U[:, a:a + 16], T.WIN[:].indirect(ucol)))
+        ucol, L = T.U[:, a + L:a + L + 1], k
+    need("s", "v", max(vU, done[0]))
+    sZ = si(s.activation(T.SZF[:], blk128(T.W, 0).indirect(ucol), FN.Copy))
+    need("v", "v", max(vU, done[0], done[ZS]))
+    a = L % 2
+    n = vi(v.tensor_copy(T.SZ[:, a:a + 16], blk128(T.W, 0).indirect(ucol)))
+    need("v", "v", n)
+    b = ZS % 2
+    n = vi(v.tensor_copy(T.S0[:, b:b + 16], blk128(T.W, ZS).indirect(T.SZ[:, a + L:a + L + 1])))
+    need("v", "v", n)
+    need("v", "s", max(sZ, sDB))
+    lists = (T.SA[:, 16:17], T.S0[:, b + ZS:b + ZS + 1])
+    vSA = vi(v.tensor_scalar(T.SA[:, 1:17], blk128(T.W, ZS + 16).indirect(lists[1]), T.PF[:, 6:7], T.SZF[:, L:L + 1],
+                             OP.mult, OP.add))
+    v.wait_ge(S.ge, 64)
+    vC, vE = {}, {}
+    for h in (1, 0):
+        need("v", "v", vSA if h == 0 else 0)
+        vC[h] = vi(v.tensor_tensor(T.CM[:, 16 * h:16 * h + 16], blk128(T.AE, 2 * h + 1).indirect(lists[h]), T.DIAGB[:], OP.add))
+        vE[h] = vi(v.tensor_tensor(T.EM[:, 16 * h:16 * h + 16], blk128(T.AE, 2 * h).indirect(lists[h]), T.MASKQ[:], OP.mult))
+    for h in (1, 0):
+        need("v", "v", vC[h])
+        vC[h] = vi(v.tensor_reduce(T.CS[:, h:h + 1], T.CM[:, 16 * h:16 * h + 16], AxisListType.X, OP.max))
+        need("v", "v", vE[h])
+        vR = vi(v.tensor_reduce(T.E2[:, h:h + 1], T.EM[:, 16 * h:16 * h + 16], AxisListType.X, OP.max))
+    need("t", "v", vC[1])
+    t.matmul(T.B6[:, 1:2], T.TRI[:], T.CS[:, 1:2], False, False)
+    t.matmul(T.B6[:, 0:1], T.BH[:], T.CS[:, 1:2], False, False)
+    t.matmul(T.B6[:, 2:3], T.BLK[:], T.CS[:, 1:2], False, False)
+    need("t", "v", vC[0])
+    t.matmul(T.B6[:, 0:1], T.TRI[:], T.CS[:, 0:1], False, False)
+    t.matmul(T.B6[:, 1:2], T.BL[:], T.CS[:, 0:1], False, False)
+    tB = ti(t.matmul(T.B6[:, 2:3], T.BLK[:], T.CS[:, 0:1], False, True))
+    for h in (1, 0):
+        need("v", "v", vC[h])
+        vi(v.tensor_scalar(T.GTB[:, 32 * h:32 * h + 32], T.MT[:], T.CS[:, h:h + 1], None, OP.is_lt))
+    need("v", "v", vR)
     vi(v.tensor_scalar(T.D[:, 0::4], T.E2[:], 63, None, OP.bitwise_and))
     for m in range(1, 4):
         vD = vi(v.tensor_scalar(T.D[:, m::4], T.E2[:], 6 * m, 63, OP.logical_shift_right, OP.bitwise_and))
-    need("v", "t", tB1)
-    vO1 = vi(v.tensor_scalar(T.OH1[:, 0:131], T.IOTAX[:, 0:131], T.B7[:, 0:1], None, OP.is_equal))
-    need("v", "v", vD)
-    vVB = vi(v.tensor_tensor(T.VB[:], T.D[:].indirect(T.REP[:]), T.GTB[:], OP.mult))
-    z = T.B1[:, 0:8]
-    for w, tile in enumerate((T.GTB, T.VB)):
-        for k in range(8):
-            need("t", "v", vVB if w else (vO1 if k > 3 else max(vO0, vG1)))
-            m = k % 4
-            ins = t.matmul(z, (T.OH0, T.OH1)[k // 4][:, 3 - m:131 - m], tile[:, 8 * k:8 * k + 8],
-                           w == 0 and k == 0, w == 1 and k == 7)
+    need("v", "gq", gALL)
+    need("v", "t", tB)
+    vN = vi(v.tensor_copy(T.CNT[:], T.B6[:, 2:3]))
+    if sends:
+        need("g", "v", vN)
+        to = T.cores[rank + 1:]
+        for part in parts(topo, T, rank)[::-1]:
+            send(part, "cn", T.CNT[:], [T.MR[:, rank:rank + 1]] * len(part))
+    for h in range(2):
+        vi(v.tensor_scalar(T.OHM[:, 70 * h:70 * h + 35], T.IOTAM[:, 0:35], T.B6[:, h:h + 1], None, OP.is_equal))
+        vO = vi(v.tensor_scalar(T.OHM[:, 70 * h + 35:70 * h + 70], T.IOTAM[:, 35:70], T.B6[:, 2:3], T.B6[:, h:h + 1],
+                                OP.add, OP.is_equal))
+        if h == 0:
+            need("v", "v", max(vD, vRP))
+            need("v", "s", sVZ)
+            vO = vi(v.tensor_tensor(T.VBZ[:, 0::16], T.D[:].indirect(T.REP[:]), T.GTB[:], OP.mult))
+        need("t", "v", vO)
+        for m in range(4):
+            ins = t.matmul(T.B5[:, 0:67], blk128(T.VBZ, 4 * h + m), T.OHM[:, 70 * h + 3 - m:70 * h + 70 - m],
+                           h + m == 0, h + m == 4)
+    tM = ti(ins)
+    for h in range(2):
+        vO = vi(v.tensor_scalar(T.OHZ[:, 100 * h:100 * h + 100], T.IOTAZ[:], T.B6[:, h:h + 1], None, OP.is_equal))
+    need("v", "s", sIO)
+    need("v", "v", vN)
+    if sends:
+        n = vi(v.tensor_scalar(T.IO[:, 4:8], T.IO[:, 4:8], T.CNT[:], None, OP.subtract))
+    else:
+        n = vO = vi(v.tensor_scalar(T.GE[:], T.IOTA[:, 0:96], T.CNT[:], -1.0, OP.is_ge, OP.mult))
+    need("v", "t", tM)
+    vM = vi(v.tensor_copy(T.MS[:, 5:72], T.B5[:, 0:67]))
+    need("g", "gq", gALL)
+    need("g", "v", vM)
+    to = beside(T, rank)
+    send([T.cores[r] for r in to], "z%d" % rank, T.MS[:], [T.WP[:, 0:72] if r > rank else T.WN[:] for r in to])
+    g.wait_ge(S.lsf, cnt["lsf"])
+    need("t", "v", vO)
+    for k in range(8):
+        a = 100 * (k // 4) + 3 - k % 4
+        ins = t.matmul(T.B7[:, 0:96], blk128(T.VBZ, k), T.OHZ[:, a:a + 96], k == 0, k == 7 and sends)
+    if not sends:
+        ins = t.matmul(T.B7[:, 0:96], T.ID[:], T.GE[:], False, True)
     tZ = ti(ins)
-    need("v", "t", tZ)
-    vZ = vi(v.tensor_copy(T.ZB[:], z))
-    need("g", "v", vZ)
-    near = beside(T, rank)
-    mask, ne = common_mask(topo, core, [T.cores[r] for r in near], MOST)
-    g.remote_dma_fused([RemoteDMATransfer(dst_ids=[dst_id(topo, T.cores[r]) for r in near], dma_engine_mask=mask,
-                                          remote_sem=S.arrz, srcs=[T.ZB[:]],
-                                          dsts=[(T.ZN if r < rank else T.ZP)[:] for r in near], alu_op=0)],
-                       local_sem=S.lsz)
-    g.wait_ge(S.lsz, ne)
-    o = T.B2[0:8, 0:64]
-    need("t", "v", vZ)
-    t.matmul(o, T.ZB[:], T.SELW[:, 64:128], True, False)
-    t.wait_ge(S.arrz, sum(common_mask(topo, T.cores[r], [T.cores[x] for x in beside(T, r)], MOST)[1] for r in near))
-    for n, r in enumerate(near):
-        c = 128 if r < rank else 0
-        ins = t.matmul(o, (T.ZP if r < rank else T.ZN)[:], T.SELW[:, c:c + 64], False, n == len(near) - 1)
-    tY = ti(ins)
-    need("v", "t", tY)
-    vY = vi(v.tensor_scalar(T.YS[0:8, :], o, -1.0, None, OP.add))
-    need("y", "v", vY)
-    y.dma_start(T.y[:], T.YS[0:8, :]).then_inc(S.st, 16)
+    need("s", "t", tZ)
+    sZ = si(s.activation(T.WP[:, 72:168], T.B7[:, 0:96], FN.Copy))
+    if rank:
+        need("v", "cn", from_parts(range(rank)))
+        n = vi(v.tensor_reduce(T.SUM[:], T.MR[:, 0:rank], AxisListType.X, OP.add))
+    need("v", "v", n)
+    n = vi(v.tensor_scalar(T.YL[:], T.IO[:], T.SUM[:] if rank else 0.0, 4.0, OP.subtract, OP.max))
+    need("v", "v", n)
+    need("v", "s", sZ)
+    if rank:
+        heard("v", rank - 1)
+    n = vi(v.tensor_copy((T.Y1 if sends else T.YS)[:], T.WP[:].indirect(T.YL[:, 0:4])))
+    if sends:
+        need("v", "v", n)
+        heard("v", rank + 1)
+        n = vi(v.tensor_tensor(T.YS[:], T.WN[:].indirect(T.YL[:, 4:8]), T.Y1[:], OP.add))
+    need("y", "v", n)
+    y.dma_start(T.y[:], T.YS[0::16, :]).then_inc(S.st, 16)
     y.wait_ge(S.st, 16)

@@ -1,14 +1,15 @@
 from concourse.mybir import dt, AluOpType, AxisListType, ActivationFunctionType
 from concourse.bass import IndirectOffsetOnAxis, DstId, RemoteDMATransfer
 
-SCRATCH = {"emd": ("dram", [512, 128], "int32"), "nxd": ("dram", [512, 128], "int32")}
+SCRATCH = {"emd": ("dram", [512, 256], "int32")}
 for _t, _l in (
     ("int32", "TN:32,16 TS:32,16 SY:128 IDX:4 IDY:2 AE:512 EM:32 E2:2 D:8 P:1 PI:8 P16:16 Q16:16"),
     ("bfloat16", "TB:32,16 TBLK:32,32 SYM:128 O:128 XS:24 XR:96 XQ:128 INJ:2048 W:4096 WS:1536 WIN:128 "
                  "CM:32 CS:2 CN:4 GTB:64 VBZ:1024 OHM:140 OHZ:200 MS:72 WP:168 WN:72 ONES:128 SC:128 L2:128 "
-                 "ID:128 BLKA:128 BLK:128 TRI:128 BH:128 BL:128 IOTA:128 IOTAM:70 IOTAZ:100 SEL:72 GE:96"),
-    ("uint16", "OFF:256 UR:8 U:288 SZ:18 S0:18 SA:18 REP:4 XL:8 YL:8"),
-    ("float32", "SZF:16 Y1:64 YS:64 PF:12 PX:1 MASKQ:16 DIAGB:16 IOR:4 IOG:8 IO0:8 IO:8 MT0:32 MT1:32 MT:32 "
+                 "ID:128 BLKA:128 BLK:128 TRI:128 BH:128 BL:128 IOTA:128 IOTAM:70 IOTAZ:100 SEL:72 GE:96 II:128 "
+                 "MASKI:128 XM:256 WA:128 WB:128 WZ:128 CW:768"),
+    ("uint16", "OFF:256 UR:8 U:128 S0:18 SA:18 REP:4 REP2:16 XL:8 YL:8 LS:16 LR:48"),
+    ("float32", "Y1:64 YS:64 PF:12 PX:1 MASKQ:16 DIAGB:16 IOR:4 IOG:16 IO0:8 IO:8 MT0:32 MT1:32 MT:32 "
                 "CNT:1 MR:8 SUM:1"),
 ):
     for _b in _l.split():
@@ -16,8 +17,8 @@ for _t, _l in (
         SCRATCH[_n] = ("sbuf", [128] + [int(_x) for _x in _d.split(",")], _t)
 for _b in range(8):
     SCRATCH["B%d" % _b] = ("psum", [128, 512], "float32")
-SEMAPHORES = ["ldsy", "ldn0", "ldn1", "ldn2", "ldn3", "ldem", "ldnx", "ldidx", "v", "t", "s", "gq", "ge",
-              "arr", "u0", "cn", "z0", "z1", "z2", "z3", "z4", "z5", "lsf", "lsz", "st"]
+SEMAPHORES = ["ldsy", "ldn0", "ldn1", "ldn2", "ldn3", "ldem", "ldidx", "v", "t", "s", "gq", "ge",
+              "arr", "lst", "u0", "cn", "z0", "z1", "z2", "z3", "z4", "z5", "lsf", "st"]
 OP = AluOpType
 FN = ActivationFunctionType
 MOST = 8
@@ -105,8 +106,8 @@ def rank_program(g, core, T, topo):
     for h, j in enumerate((0, ZS + 1, 16)):
         y.dma_start(T.IDX[:, h:h + 1], T.sy[:, j:j + 16]).then_inc(S.ldidx, 16)
     y.wait_ge(S.ldn2, 16)
-    y.dma_start(T.emd[:], T.em[:]).then_inc(S.ldem, 16)
-    y.dma_start(T.nxd[:], T.nx[:]).then_inc(S.ldnx, 16)
+    y.dma_start(T.emd[:, 0:128], T.em[:]).then_inc(S.ldem, 16)
+    y.dma_start(T.emd[:, 128:256], T.nx[:]).then_inc(S.ldem, 16)
 
     gP16 = gi(g.iota(T.P16[:], [[-1, 16]], 16, 1))
     gP = gi(g.iota(T.P[:], [[1, 1]], 0, 4))
@@ -114,6 +115,8 @@ def rank_program(g, core, T, topo):
     v_ones = vi(v.memset(T.ONES[:], 1.0))
     need("g", "v", v_ones)
     gL2 = gi(g.affine_select(T.L2[0:2, :], T.ONES[0:2, :], [[1, 2], [0, 64]], OP.is_equal, 0.0, 0, -1))
+    iota(T.II[:], [[0, 8], [1, 16]], 0)
+    gII = iota(T.IOG[:], [[1, 2], [3, 8]], 0)
     vi(v.memset(T.TBLK[:], 0.0))
     need("v", "gq", gP)
     vi(v.tensor_scalar(T.PI[:, 3:4], T.P[:], 2, 63, OP.logical_shift_right, OP.bitwise_and))
@@ -188,23 +191,25 @@ def rank_program(g, core, T, topo):
     n1 = vi(v.tensor_scalar(T.PF[:, 7:8], T.IDX[:, 2:3], T.PF[:, 6:7], T.PF[:, 1:2], OP.mult, OP.add))
     vi(v.tensor_scalar(T.IDY[:, 1:2], T.IDX[:, 1:2], T.PF[:, 1:2], None, OP.add))
     vQ3 = vi(v.tensor_scalar(T.PF[:, 8:9], T.PI[:, 4:5], 21.0, T.PF[:, 0:1], OP.mult, OP.add))
+    need("v", "gq", gII)
+    vi(v.tensor_scalar(T.MASKI[:], T.II[:], T.PF[:, 0:1], 128.0, OP.is_equal, OP.mult))
+    need("v", "v", n1)
+    vID = vi(v.tensor_scalar(T.IDY[:, 0:1], T.IDX[:, 0:1], T.PF[:, 5:6], T.PF[:, 7:8], OP.mult, OP.add))
     for q in V_THEN[1:]:
         inj_v(q)
     need("v", "t", tOFF)
     vOA = vi(v.tensor_copy(T.OFF[:, 8 * BS:256], T.B1[:, 8 * BS:256]))
     vOB = vi(v.tensor_copy(T.OFF[:, 0:8 * BS], T.B1[:, 0:8 * BS]))
-    need("v", "v", n1)
-    vID = vi(v.tensor_scalar(T.IDY[:, 0:1], T.IDX[:, 0:1], T.PF[:, 5:6], T.PF[:, 7:8], OP.mult, OP.add))
+    vi(v.tensor_copy(T.REP2[:], T.IOG[:]))
     sB = 0
     rows = list(S_CHAIN)
-    if sends:
-        need("s", "v", vOB)
-        for j in range(BS - 1, -1, -1):
-            need("s", "s", sB)
-            win = T.IOTA[:] if j == BS - 1 else blk128(T.WS, j + 1)
-            sB = si(s.activation(blk128(T.WS, j), win.indirect(T.OFF[:, 8 * j:8 * j + 8]), FN.Copy))
-            if rows and j:
-                inj_s(rows.pop(0))
+    need("s", "v", vOB)
+    for j in range(BS - 1, -1, -1):
+        need("s", "s", sB)
+        win = T.IOTA[:] if j == BS - 1 else blk128(T.WS, j + 1)
+        sB = si(s.activation(blk128(T.WS, j), win.indirect(T.OFF[:, 8 * j:8 * j + 8]), FN.Copy))
+        if rows and j:
+            inj_s(rows.pop(0))
     for q in rows + list(S_LAST):
         inj_s(q)
 
@@ -236,29 +241,22 @@ def rank_program(g, core, T, topo):
     gi(g.affine_select(T.SEL[:, 0:48], T.ONES[:, 0:48], [[-2000, 2], [-16, 8], [1000, 3]], OP.is_equal, 0.0, 0, 1))
     gi(g.affine_select(T.SEL[:, 48:72], T.ONES[:, 0:24], [[-16, 8], [1000, 3]], OP.is_equal, 0.0, -1015, 1))
     n2 = gi(g.affine_select(T.SC[:], T.ONES[:], [[0, 128]], OP.is_gt, 1.0 / 128, 0, 0))
-    n3 = iota(T.MT0[:], [[128, 4], [0, 8]], 128 * 129)
+    iota(T.IOR[:], [[2, 4]], 0)
     need("g", "gq", n2)
     n2 = gi(g.affine_select(T.BLKA[:], T.SC[:], [[-16, 8], [0, 16]], OP.is_ge, 0.0, 0, 1))
     gi(g.affine_select(T.ID[:], T.ONES[:], [[1, 128]], OP.is_equal, 0.0, 0, -1))
     need("g", "gq", n2)
-    n2 = gi(g.affine_select(T.BLK[:], T.BLKA[:], [[16, 8], [0, 16]], OP.is_ge, 0.0, 15, -1))
-    n3 = gi(g.affine_select(T.MT1[:], T.MT0[:], [[0, 4], [-16, 8]], OP.is_ge, 1e6, 0, 1))
-    iota(T.IOR[:], [[2, 4]], 0)
-    iota(T.IOG[:], [[3, 8]], 0)
-    need("g", "gq", n3)
-    gi(g.affine_select(T.MT[:], T.MT1[:], [[0, 4], [16, 8]], OP.is_ge, 1e6, 15, -1))
-    gi(g.affine_select(T.TRI[:], T.BLK[:], [[1, 128]], OP.is_gt, 0.0, 0, -1))
-    gC = iota(T.IO0[:], [[-67, 2], [16, 4]], 64 * rank + 72)
+    gC = gi(g.affine_select(T.BLK[:], T.BLKA[:], [[16, 8], [0, 16]], OP.is_ge, 0.0, 15, -1))
     need("g", "v", vID)
 
-    def fetch(w):
-        need("g", ("ldem", "ldnx")[w], 16)
-        for h in range(2):
-            g.indirect_dma_start(blk128(T.AE, 2 * h + w), None, (T.emd, T.nxd)[w][:],
-                                 IndirectOffsetOnAxis(ap=T.IDY[:, h:h + 1], axis=0), bounds_check=511).then_inc(S.ge, 16)
-
-    fetch(0)
-    need("t", "gq", gC)
+    n3 = iota(T.MT0[:], [[128, 4], [0, 8]], 128 * 129)
+    gIO = iota(T.IO0[:], [[-67, 2], [16, 4]], 64 * rank + 72)
+    need("g", "gq", n3)
+    n3 = gi(g.affine_select(T.MT1[:], T.MT0[:], [[0, 4], [-16, 8]], OP.is_ge, 1e6, 0, 1))
+    need("g", "ldem", 32)
+    for h in range(2):
+        g.indirect_dma_start(T.AE[:, 256 * h:256 * h + 256], None, T.emd[:],
+                             IndirectOffsetOnAxis(ap=T.IDY[:, h:h + 1], axis=0), bounds_check=511).then_inc(S.ge, 16)
     if rank == 0:
         need("v", "v", done[BS])
         n = vi(v.tensor_copy(T.U[:, 18:34], blk128(T.W, BS).indirect(T.U[:, 0:1])))
@@ -268,25 +266,48 @@ def rank_program(g, core, T, topo):
         need("g", "v", n)
         for part in parts(topo, T, rank):
             send(part, "u0", T.U[:, 52:54], [T.UR[:, 0:2]] * len(part))
-    elif sends:
-        o = T.B2[:, 0:24]
-        need("t", "v", done[BS])
-        t.matmul(o, blk128(T.W, BS), T.SEL[:, 48:72], True, False)
-        need("t", "s", sB)
-        t.matmul(o, blk128(T.WS, 0), T.SEL[:, 0:24], False, False)
-        need("t", "v", done[ZS + 16])
-        tX = ti(t.matmul(o, blk128(T.W, ZS + 16), T.SEL[:, 24:48], False, True))
-        step(later.pop(0))
-        step(later.pop(0))
-        need("v", "t", tX)
-        vX = vi(v.tensor_copy(T.XS[:], o))
+    o = T.B2[:, 0:24]
+    need("t", "gq", gC)
+    need("t", "v", done[BS])
+    t.matmul(o, blk128(T.W, BS), T.SEL[:, 48:72], True, False)
+    need("t", "s", sB)
+    t.matmul(o, blk128(T.WS, 0), T.SEL[:, 0:24], False, False)
+    need("t", "v", done[ZS + 16])
+    tX = ti(t.matmul(o, blk128(T.W, ZS + 16), T.SEL[:, 24:48], False, True))
+    step(later.pop(0))
+    step(later.pop(0))
+    need("v", "gq", gC)
+    vRP = vi(v.tensor_scalar(T.REP[:], T.IOR[:], T.PF[:, 2:3], None, OP.add))
+    wide = 24 * (rank - 1)
+    if rank > 1:
+        vXL = vi(v.tensor_scalar(T.XL[:], T.IOG[:, 0:8], T.PF[:, 8:9], wide - 1.0, OP.add, OP.min))
+    need("v", "t", tX)
+    vX = vi(v.tensor_copy(T.XS[:], o))
+    if rank and sends:
         need("g", "v", vX)
         for part in parts(topo, T, rank):
             send(part, "arr", T.XS[:], [T.XR[:, 24 * rank - 24:24 * rank]] * len(part))
-    fetch(1)
+    step(later.pop(0))
+    need("v", "v", vX)
+    for k in (1, 0):
+        n = vi(v.tensor_tensor(blk128(T.XM, k), T.XS[:].indirect(T.REP2[:, 8 * k:8 * k + 8]), T.MASKI[:], OP.mult))
+        need("t", "v", n)
+        m = t.matmul(T.B3[:, 8 * k:8 * k + 8], blk128(T.XM, k), T.BLK[:, 0::16], True, True)
+    tL = ti(m)
+    step(later.pop(0))
+    step(later.pop(0))
+    need("v", "t", tL)
+    vL = vi(v.tensor_copy(T.LS[:], T.B3[:, 0:16]))
+    if rank > 1 and sends:
+        need("g", "v", vL)
+        for part in parts(topo, T, rank):
+            send(part, "lst", T.LS[:], [T.LR[:, 16 * rank - 32:16 * rank - 16]] * len(part))
+    need("g", "gq", n3)
+    gi(g.affine_select(T.TRI[:], T.BLK[:], [[1, 128]], OP.is_gt, 0.0, 0, -1))
     gi(g.affine_select(T.BH[:], T.BLK[:], [[0, 8], [1, 16]], OP.is_ge, 0.0, -ZS - 1, 0))
     gi(g.affine_select(T.BL[:], T.BLK[:], [[16, 8], [0, 16]], OP.is_ge, 0.0, ZS, -1))
-    iota(T.CN[:], [[16512, 2], [0, 2]], -16512)
+    gT = iota(T.CN[:], [[16512, 2], [0, 2]], -16512)
+    gi(g.affine_select(T.MT[:], T.MT1[:], [[0, 4], [16, 8]], OP.is_ge, 1e6, 15, -1))
     iota(T.IOTAM[:], [[-32, 2], [1, 35]], -3)
     iota(T.IOTAZ[:], [[1, 100]], -3)
     iota(T.MS[:, 0:5], [[0, 5]], 0)
@@ -295,20 +316,20 @@ def rank_program(g, core, T, topo):
     gALL = cnt["gq"]
     for j in later:
         step(j)
-    sDB = si(s.activation(T.DIAGB[:], T.MASKQ[:], FN.Copy, scale=16448.5))
     need("s", "s", inj[1][1])
     sVZ = si(s.activation(T.VBZ[:], T.INJ[:, 0:1024], FN.Copy, scale=0.0))
-    need("s", "gq", gC)
-    need("s", "v", vOB)
+    need("s", "v", vL)
+    n = si(s.activation(T.WA[:], blk128(T.W, ZS + 16).indirect(T.LS[:, 8:16]), FN.Copy))
+    sDB = si(s.activation(T.DIAGB[:], T.MASKQ[:], FN.Copy, scale=16448.5))
+    need("s", "s", n)
+    sWB = si(s.activation(T.WB[:], T.WA[:].indirect(T.LS[:, 0:8]), FN.Copy, scale=T.PF[:, 6:7]))
+    need("s", "gq", gIO)
     sIO = si(s.activation(T.IO[:], T.IO0[:], FN.Identity, bias=T.PF[:, 0:1]))
-    need("v", "gq", gC)
-    vRP = vi(v.tensor_scalar(T.REP[:], T.IOR[:], T.PF[:, 2:3], None, OP.add))
     ucol, L, vU = T.UR[:, 0:1], 0, 0
     if rank == 0:
         vU = vi(v.memset(T.UR[:], 0))
+    made = {}
     if rank > 1:
-        wide = 24 * (rank - 1)
-        vXL = vi(v.tensor_scalar(T.XL[:], T.IOG[:], T.PF[:, 8:9], wide - 1.0, OP.add, OP.min))
         for q in "vs":
             need(q, "v", vXL)
             need(q, "arr", from_parts(range(1, rank)))
@@ -317,80 +338,94 @@ def rank_program(g, core, T, topo):
         need("t", "v", vQ)
         need("t", "s", sQ)
         tW = ti(t.matmul(T.B4[:, 0:128], T.XQ[:], T.ID[:], True, True))
+    need("v", "s", sWB)
+    need("v", "v", done[0])
+    vJ = vi(v.tensor_tensor(T.WZ[:], T.WB[:], blk128(T.W, 0), OP.add))
+    if rank > 1:
         need("v", "t", tW)
-        vU = vi(v.tensor_copy(T.WIN[:], T.B4[:, 0:128]))
-    need("t", "gq", gALL)
+        vU = vW = vi(v.tensor_copy(T.WIN[:], T.B4[:, 0:128]))
+
+    def compose(q, r, k):
+        need(q, "v", vW)
+        need(q, "lst", from_parts(range(2, rank)))
+        if k == 0:
+            need(q, q, made[r])
+        win = (T.WIN[:] if k else blk128(T.CW, 2 * r - 3)).indirect(T.LR[:, 16 * r - 32 + 8 * k:16 * r - 24 + 8 * k])
+        o = blk128(T.CW, 2 * r - 4 + k)
+        made[r] = vi(v.tensor_copy(o, win)) if q == "v" else si(s.activation(o, win, FN.Copy))
+
+    for k in (1, 0):
+        for r in range(2, min(rank, 4)):
+            compose("s", r, k)
+    need("t", "gq", gT)
     t.matmul(T.B6[:, 0:3], T.TRI[:], T.CN[:, 0:3], True, False)
     for col, mat in ((0, T.BH), (1, T.BL), (2, T.BLK), (2, T.BLK)):
         t.matmul(T.B6[:, col:col + 1], mat[:], T.CN[:, 0:1], False, False)
     if rank:
         need("v", "u0", from_parts([0]))
-        need("s", "u0", from_parts([0]))
-    for k in range(3 * rank - 3):
+    hops = [(T.WIN[:], k, 0) for k in range(3)] + [(blk128(T.CW, 2 * r - 4), 3 * r - 1, r) for r in range(2, rank)]
+    for k, (win, valid, r) in enumerate(hops if rank > 1 else []):
         a = 18 * k + L % 2
         need("v", "v", vU)
-        vU = vi(v.tensor_copy(T.U[:, a:a + 16], T.WIN[:].indirect(ucol)))
-        ucol, L = T.U[:, a + L:a + L + 1], k
-    need("s", "v", max(vU, done[0]))
-    sZ = si(s.activation(T.SZF[:], blk128(T.W, 0).indirect(ucol), FN.Copy))
-    need("v", "v", max(vU, done[0], done[ZS]))
-    a = L % 2
-    n = vi(v.tensor_copy(T.SZ[:, a:a + 16], blk128(T.W, 0).indirect(ucol)))
+        if r:
+            need("v", "sv"[r // 4], made[r])
+        vU = vi(v.tensor_copy(T.U[:, a:a + 16], win.indirect(ucol)))
+        ucol, L = T.U[:, a + L:a + L + 1], valid
+        if rank > 4 and k < 2:
+            compose("v", 4, 1 - k)
+    need("v", "v", max(vU, vJ, done[ZS]))
+    a, b = L % 2, ZS % 2
+    lists = (T.SA[:, a + L:a + L + 1], T.S0[:, b + ZS:b + ZS + 1])
+    n = vi(v.tensor_copy(T.SA[:, a:a + 16], T.WZ[:].indirect(ucol)))
     need("v", "v", n)
-    b = ZS % 2
-    n = vi(v.tensor_copy(T.S0[:, b:b + 16], blk128(T.W, ZS).indirect(T.SZ[:, a + L:a + L + 1])))
-    need("v", "v", n)
-    need("v", "s", max(sZ, sDB))
-    lists = (T.SA[:, 16:17], T.S0[:, b + ZS:b + ZS + 1])
-    vSA = vi(v.tensor_scalar(T.SA[:, 1:17], blk128(T.W, ZS + 16).indirect(lists[1]), T.PF[:, 6:7], T.SZF[:, L:L + 1],
-                             OP.mult, OP.add))
-    v.wait_ge(S.ge, 64)
+    vS = vi(v.tensor_copy(T.S0[:, b:b + 16], blk128(T.W, ZS).indirect(lists[0])))
+    need("v", "s", sDB)
+    v.wait_ge(S.ge, 32)
     vC, vE = {}, {}
-    for h in (1, 0):
-        need("v", "v", vSA if h == 0 else 0)
+    for h in range(2):
+        need("v", "v", vS if h else 0)
         vC[h] = vi(v.tensor_tensor(T.CM[:, 16 * h:16 * h + 16], blk128(T.AE, 2 * h + 1).indirect(lists[h]), T.DIAGB[:], OP.add))
         vE[h] = vi(v.tensor_tensor(T.EM[:, 16 * h:16 * h + 16], blk128(T.AE, 2 * h).indirect(lists[h]), T.MASKQ[:], OP.mult))
-    for h in (1, 0):
+    for h in range(2):
         need("v", "v", vC[h])
         vC[h] = vi(v.tensor_reduce(T.CS[:, h:h + 1], T.CM[:, 16 * h:16 * h + 16], AxisListType.X, OP.max))
         need("v", "v", vE[h])
         vR = vi(v.tensor_reduce(T.E2[:, h:h + 1], T.EM[:, 16 * h:16 * h + 16], AxisListType.X, OP.max))
-    need("t", "v", vC[1])
-    t.matmul(T.B6[:, 1:2], T.TRI[:], T.CS[:, 1:2], False, False)
-    t.matmul(T.B6[:, 0:1], T.BH[:], T.CS[:, 1:2], False, False)
-    t.matmul(T.B6[:, 2:3], T.BLK[:], T.CS[:, 1:2], False, False)
-    need("t", "v", vC[0])
-    t.matmul(T.B6[:, 0:1], T.TRI[:], T.CS[:, 0:1], False, False)
-    t.matmul(T.B6[:, 1:2], T.BL[:], T.CS[:, 0:1], False, False)
-    tB = ti(t.matmul(T.B6[:, 2:3], T.BLK[:], T.CS[:, 0:1], False, True))
-    for h in (1, 0):
+    for h in range(2):
+        need("t", "v", vC[h])
+        t.matmul(T.B6[:, h:h + 1], T.TRI[:], T.CS[:, h:h + 1], False, False)
+        t.matmul(T.B6[:, 1 - h:2 - h], (T.BL, T.BH)[h][:], T.CS[:, h:h + 1], False, False)
+        m = t.matmul(T.B6[:, 2:3], T.BLK[:], T.CS[:, h:h + 1], False, h == 1)
+    tB = ti(m)
+    need("v", "gq", gALL)
+    for h in range(2):
         need("v", "v", vC[h])
         vi(v.tensor_scalar(T.GTB[:, 32 * h:32 * h + 32], T.MT[:], T.CS[:, h:h + 1], None, OP.is_lt))
     need("v", "v", vR)
     vi(v.tensor_scalar(T.D[:, 0::4], T.E2[:], 63, None, OP.bitwise_and))
     for m in range(1, 4):
         vD = vi(v.tensor_scalar(T.D[:, m::4], T.E2[:], 6 * m, 63, OP.logical_shift_right, OP.bitwise_and))
-    need("v", "gq", gALL)
     need("v", "t", tB)
-    vN = vi(v.tensor_copy(T.CNT[:], T.B6[:, 2:3]))
-    if sends:
-        need("g", "v", vN)
-        to = T.cores[rank + 1:]
-        for part in parts(topo, T, rank)[::-1]:
-            send(part, "cn", T.CNT[:], [T.MR[:, rank:rank + 1]] * len(part))
+    wide, head = (67, 35) if sends else (35, 38)
     for h in range(2):
-        vi(v.tensor_scalar(T.OHM[:, 70 * h:70 * h + 35], T.IOTAM[:, 0:35], T.B6[:, h:h + 1], None, OP.is_equal))
-        vO = vi(v.tensor_scalar(T.OHM[:, 70 * h + 35:70 * h + 70], T.IOTAM[:, 35:70], T.B6[:, 2:3], T.B6[:, h:h + 1],
-                                OP.add, OP.is_equal))
+        vO = vi(v.tensor_scalar(T.OHM[:, 70 * h:70 * h + head], T.IOTAM[:, 0:head], T.B6[:, h:h + 1], None, OP.is_equal))
+        if sends:
+            vO = vi(v.tensor_scalar(T.OHM[:, 70 * h + 35:70 * h + 70], T.IOTAM[:, 35:70], T.B6[:, 2:3], T.B6[:, h:h + 1],
+                                    OP.add, OP.is_equal))
         if h == 0:
             need("v", "v", max(vD, vRP))
             need("v", "s", sVZ)
             vO = vi(v.tensor_tensor(T.VBZ[:, 0::16], T.D[:].indirect(T.REP[:]), T.GTB[:], OP.mult))
         need("t", "v", vO)
         for m in range(4):
-            ins = t.matmul(T.B5[:, 0:67], blk128(T.VBZ, 4 * h + m), T.OHM[:, 70 * h + 3 - m:70 * h + 70 - m],
+            ins = t.matmul(T.B5[:, 0:wide], blk128(T.VBZ, 4 * h + m), T.OHM[:, 70 * h + 3 - m:70 * h + 3 - m + wide],
                            h + m == 0, h + m == 4)
     tM = ti(ins)
+    vN = vi(v.tensor_copy(T.CNT[:], T.B6[:, 2:3]))
+    if sends:
+        need("g", "v", vN)
+        for part in parts(topo, T, rank)[::-1]:
+            send(part, "cn", T.CNT[:], [T.MR[:, rank:rank + 1]] * len(part))
     for h in range(2):
         vO = vi(v.tensor_scalar(T.OHZ[:, 100 * h:100 * h + 100], T.IOTAZ[:], T.B6[:, h:h + 1], None, OP.is_equal))
     need("v", "s", sIO)
@@ -400,11 +435,12 @@ def rank_program(g, core, T, topo):
     else:
         n = vO = vi(v.tensor_scalar(T.GE[:], T.IOTA[:, 0:96], T.CNT[:], -1.0, OP.is_ge, OP.mult))
     need("v", "t", tM)
-    vM = vi(v.tensor_copy(T.MS[:, 5:72], T.B5[:, 0:67]))
+    vM = vi(v.tensor_copy(T.MS[:, 5:5 + wide], T.B5[:, 0:wide]))
     need("g", "gq", gALL)
     need("g", "v", vM)
     to = beside(T, rank)
-    send([T.cores[r] for r in to], "z%d" % rank, T.MS[:], [T.WP[:, 0:72] if r > rank else T.WN[:] for r in to])
+    send([T.cores[r] for r in to], "z%d" % rank, T.MS[:, 0:5 + wide],
+         [(T.WP if r > rank else T.WN)[:, 0:5 + wide] for r in to])
     g.wait_ge(S.lsf, cnt["lsf"])
     need("t", "v", vO)
     for k in range(8):
@@ -428,7 +464,7 @@ def rank_program(g, core, T, topo):
     if sends:
         need("v", "v", n)
         heard("v", rank + 1)
-        n = vi(v.tensor_tensor(T.YS[:], T.WN[:].indirect(T.YL[:, 4:8]), T.Y1[:], OP.add))
+        n = vi(v.tensor_tensor(T.YS[:], T.WN[:, 0:40].indirect(T.YL[:, 4:8]), T.Y1[:], OP.add))
     need("y", "v", n)
     y.dma_start(T.y[:], T.YS[0::16, :]).then_inc(S.st, 16)
     y.wait_ge(S.st, 16)

@@ -4,12 +4,12 @@ from concourse.bass import IndirectOffsetOnAxis, DstId, RemoteDMATransfer
 SCRATCH = {"emd": ("dram", [512, 256], "int32")}
 for _t, _l in (
     ("int32", "TN:32,16 TS:32,16 SY:128 IDX:4 IDY:2 AE:512 EM:32 E2:2 D:8 P:1 PI:8 P16:16 Q16:16"),
-    ("bfloat16", "TB:32,16 TBLK:32,32 SYM:128 O:128 XS:24 XR:96 XQ:128 INJ:2048 W:4096 WS:1536 WIN:128 "
-                 "CM:32 CS:2 CN:4 GTB:64 VBZ:1024 OHM:140 OHZ:200 MS:72 WP:168 WN:72 ONES:128 SC:128 L2:128 "
-                 "ID:128 BLKA:128 BLK:128 TRI:128 BH:128 BL:128 IOTA:128 IOTAM:70 IOTAZ:100 SEL:72 GE:96 II:128 "
-                 "MASKI:128 XM:256 WA:128 WB:128 WZ:128 CW:768"),
-    ("uint16", "OFF:256 UR:8 U:128 S0:18 SA:18 REP:4 REP2:16 XL:8 YL:8 LS:16 LR:48"),
-    ("float32", "Y1:64 YS:64 PF:12 PX:1 MASKQ:16 DIAGB:16 IOR:4 IOG:16 IO0:8 IO:8 MT0:32 MT1:32 MT:32 "
+    ("bfloat16", "TBLK:32,32 SYM:128 O:128 INJ:2048 W:4096 WS:1536 PW:480 TT:864 "
+                 "CM:32 CS:2 CN:2 GTB:64 VBZ:1024 OHM:140 OHZ:200 MS:72 WP:160 ONES:128 SC:128 L2:128 "
+                 "ID:128 BLKA:128 BLK:128 TRI:128 BH:128 BL:128 IOTA:128 IOTAM:70 IOTAZ:100 GE:96 "
+                 "WA:128 WB:128 CW:1536"),
+    ("uint16", "OFF:256 UR:8 U:128 S0:18 SA:18 REP:4 YL:4 TL:4 LS:32 LR:96"),
+    ("float32", "UF:16 IP:8 GAP:1 YS:64 PF:16 PX:1 MASKQ:16 DIAGB:16 IOR:4 IO0:8 IO:8 MT0:32 MT1:32 MT:32 "
                 "CNT:1 MR:8 SUM:1"),
 ):
     for _b in _l.split():
@@ -18,24 +18,31 @@ for _t, _l in (
 for _b in range(8):
     SCRATCH["B%d" % _b] = ("psum", [128, 512], "float32")
 SEMAPHORES = ["ldsy", "ldn0", "ldn1", "ldn2", "ldn3", "ldem", "ldidx", "v", "t", "s", "gq", "ge",
-              "arr", "lst", "u0", "cn", "z0", "z1", "z2", "z3", "z4", "z5", "lsf", "st"]
+              "arr1", "arr2", "arr3", "arr4", "lst1", "lst2", "lst3", "lst4", "u0", "cn",
+              "z", "lsf", "st", "ib"]
 OP = AluOpType
 FN = ActivationFunctionType
-MOST = 8
-ZS = 5
-BS = 2 * ZS
-S_FIRST, V_FIRST, S_THEN, V_THEN, S_CHAIN, S_LAST = (0, 15), (14, 13), (12, 11), (10, 9), (8, 7, 6, 5, 4, 3), (2, 1)
+ZS = 6
+BS = 12
+S_FIRST, V_FIRST, S_THEN, V_THEN, S_CHAIN, S_LAST = (0, 15), (14,), (12, 11, 10), (13, 9, 8), (), ()
+BY_DMA = 7
+MAKES = (("s", 1, 0), ("s", 2, 0), ("s", 1, 1), ("s", 2, 1), ("v", 3, 0), ("v", 4, 0), ("s", 3, 1), ("s", 4, 1),
+         ("v", 1, 2), ("v", 2, 2), ("s", 3, 2), ("s", 4, 2))
+V_LEFT = 2
 
 
-def common_mask(topo, src, dsts, most):
-    ok = [e for e in topo.engines(src, dsts[0]) if all(e in topo.engines(src, d) for d in dsts)][:most]
-    return sum(1 << e for e in ok), len(ok)
+def deal(topo, T, r, to, how="out"):
+    me = T.cores[r]
+    away = [x for x in range(len(T.cores)) if topo.chip(T.cores[x]) != topo.chip(me)]
+    mate = [x for x in range(len(T.cores)) if x not in away and x != r][0]
+    out = [e for e in topo.engines(me, T.cores[away[0]]) if all(e in topo.engines(me, T.cores[x]) for x in away)]
+    rest = [e for e in topo.engines(me, T.cores[mate]) if e not in out]
+    first = [x for x in to if x in away] or {"out": to, "rest": [], "both": to[:1]}[how]
+    return [p for p in ((first, out), ([x for x in to if x not in first], rest)) if p[0]]
 
 
-def parts(topo, T, r):
-    me, later = T.cores[r], T.cores[r + 1:][::-1]
-    two = ([d for d in later if topo.chip(d) != topo.chip(me)], [d for d in later if topo.chip(d) == topo.chip(me)])
-    return [p for p in two if p]
+def after(T, r):
+    return list(range(len(T.cores) - 1, r, -1))
 
 
 def beside(T, r):
@@ -81,17 +88,17 @@ def rank_program(g, core, T, topo):
             queues[q].wait_ge(S[key], n)
             seen[(q, key)] = n
 
-    def send(cores, sem, src, dsts):
-        mask, ne = common_mask(topo, core, cores, MOST)
-        g.remote_dma_fused([RemoteDMATransfer(dst_ids=[dst_id(topo, d) for d in cores], dma_engine_mask=mask,
-                                              remote_sem=S[sem], srcs=[src], dsts=dsts, alu_op=0)], local_sem=S.lsf)
-        cnt["lsf"] += ne
+    def transfer(ranks, engines, sem, src, dst):
+        cnt["lsf"] += len(engines)
+        return RemoteDMATransfer(dst_ids=[dst_id(topo, T.cores[x]) for x in ranks], dma_engine_mask=sum(1 << e for e in engines),
+                                 remote_sem=S[sem], srcs=[src], dsts=[dst] * len(ranks), alu_op=0)
 
-    def from_parts(ranks):
-        return sum(common_mask(topo, T.cores[r], p, MOST)[1] for r in ranks for p in parts(topo, T, r) if core in p)
+    def send(to, sem, src, dst, how="out"):
+        for ranks, engines in deal(topo, T, rank, to, how):
+            g.remote_dma_fused([transfer(ranks, engines, sem, src, dst)], local_sem=S.lsf)
 
-    def heard(q, r):
-        need(q, "z%d" % r, common_mask(topo, T.cores[r], [T.cores[x] for x in beside(T, r)], MOST)[1])
+    def from_parts(senders, to=after, how="out"):
+        return sum(len(engines) for r in senders for ranks, engines in deal(topo, T, r, to(T, r), how) if rank in ranks)
 
     def iota(out, pattern, base, cm=0):
         return gi(g.iota(out, pattern, base, cm, allow_small_or_imprecise_dtypes=True))
@@ -105,9 +112,6 @@ def rank_program(g, core, T, topo):
         (y, s)[i % 2].dma_start(T.TN[:, 8 * i:8 * i + 8, :], T.nx[2 * i:2 * i + 2, :]).then_inc(S["ldn%d" % i], 16)
     for h, j in enumerate((0, ZS + 1, 16)):
         y.dma_start(T.IDX[:, h:h + 1], T.sy[:, j:j + 16]).then_inc(S.ldidx, 16)
-    y.wait_ge(S.ldn2, 16)
-    y.dma_start(T.emd[:, 0:128], T.em[:]).then_inc(S.ldem, 16)
-    y.dma_start(T.emd[:, 128:256], T.nx[:]).then_inc(S.ldem, 16)
 
     gP16 = gi(g.iota(T.P16[:], [[-1, 16]], 16, 1))
     gP = gi(g.iota(T.P[:], [[1, 1]], 0, 4))
@@ -115,8 +119,15 @@ def rank_program(g, core, T, topo):
     v_ones = vi(v.memset(T.ONES[:], 1.0))
     need("g", "v", v_ones)
     gL2 = gi(g.affine_select(T.L2[0:2, :], T.ONES[0:2, :], [[1, 2], [0, 64]], OP.is_equal, 0.0, 0, -1))
-    iota(T.II[:], [[0, 8], [1, 16]], 0)
-    gII = iota(T.IOG[:], [[1, 2], [3, 8]], 0)
+    y.wait_ge(S.ldn0, 16)
+    y.dma_start(T.emd[:, 0:128], T.em[:]).then_inc(S.ldem, 16)
+    y.dma_start(T.emd[:, 128:256], T.nx[:]).then_inc(S.ldem, 16)
+    gPW = iota(T.PW[:], [[0, 480]], 0)
+    inj = {}
+    need("y", "gq", iota(T.INJ[:, 128:128 + 128 * BY_DMA], [[0, 128 * BY_DMA]], 0))
+    for q in range(BY_DMA, 0, -1):
+        y.dma_start(T.INJ[q::16, 128 * q:128 * q + 128], T.IOTA[q::16, :]).then_inc(S.ib, 16)
+        inj[q] = ("ib", 16 * BY_DMA)
     vi(v.memset(T.TBLK[:], 0.0))
     need("v", "gq", gP)
     vi(v.tensor_scalar(T.PI[:, 3:4], T.P[:], 2, 63, OP.logical_shift_right, OP.bitwise_and))
@@ -127,7 +138,8 @@ def rank_program(g, core, T, topo):
     need("v", "v", n)
     vMQ = vi(v.tensor_scalar(T.MASKQ[:], T.Q16[:], 0.0, None, OP.is_equal))
     vPX = vi(v.tensor_copy(T.PX[:], T.PI[:, 3:4]))
-    inj = {}
+    for c, bits in ((5, 24), (6, 4), (7, 64)):
+        vi(v.tensor_scalar(T.PI[:, c:c + 1], T.P[:], bits, None, OP.bitwise_and))
 
     def inj_v(q):
         need("v", "gq", gI)
@@ -159,8 +171,11 @@ def rank_program(g, core, T, topo):
         r8 = slice(8 * i, 8 * i + 8)
         need("v", "v", vTS[i])
         need("s", "v", vTS[i])
-        blk[i] = (vi(v.tensor_copy(T.TBLK[0:64, r8, 0:16], T.TS[0:64, r8, :])),
-                  si(s.activation(T.TBLK[64:128, r8, 16:32], T.TS[64:128, r8, :], FN.Copy)))
+        n = vi(v.tensor_copy(T.TBLK[0:64, r8, 0:16], T.TS[0:64, r8, :]))
+        if i == 3:
+            n = vi(v.tensor_copy(T.TBLK[64:128, 24:27, 16:32], T.TS[64:128, 24:27, :]))
+            r8 = slice(27, 32)
+        blk[i] = (n, si(s.activation(T.TBLK[64:128, r8, 16:32], T.TS[64:128, r8, :], FN.Copy)))
 
     states(0)
     states(1)
@@ -183,33 +198,51 @@ def rank_program(g, core, T, topo):
         inj_s(q)
     vi(v.tensor_copy(T.PF[:, 0:3], T.PI[:, 0:3]))
     vi(v.tensor_scalar(T.PF[:, 5:6], T.PI[:, 0:1], ZS + 0.5, None, OP.is_lt))
-    vi(v.tensor_scalar(T.PF[:, 6:7], T.PI[:, 0:1], ZS + 0.5, None, OP.is_gt))
-    n1 = vi(v.tensor_scalar(T.PI[:, 4:5], T.PI[:, 0:1], -1.0, 1.0 / 3, OP.add, OP.mult))
-    inj_v(V_THEN[0])
+    n1 = vi(v.tensor_scalar(T.PF[:, 6:7], T.PI[:, 0:1], ZS + 0.5, None, OP.is_gt))
+    for q in V_THEN[:2]:
+        inj_v(q)
     need("v", "ldidx", 48)
     need("v", "v", n1)
     n1 = vi(v.tensor_scalar(T.PF[:, 7:8], T.IDX[:, 2:3], T.PF[:, 6:7], T.PF[:, 1:2], OP.mult, OP.add))
     vi(v.tensor_scalar(T.IDY[:, 1:2], T.IDX[:, 1:2], T.PF[:, 1:2], None, OP.add))
-    vQ3 = vi(v.tensor_scalar(T.PF[:, 8:9], T.PI[:, 4:5], 21.0, T.PF[:, 0:1], OP.mult, OP.add))
-    need("v", "gq", gII)
-    vi(v.tensor_scalar(T.MASKI[:], T.II[:], T.PF[:, 0:1], 128.0, OP.is_equal, OP.mult))
+    vi(v.tensor_scalar(T.PF[:, 3:4], T.PI[:, 5:6], 4.0, None, OP.mult))
+    for q in V_THEN[2:]:
+        inj_v(q)
     need("v", "v", n1)
     vID = vi(v.tensor_scalar(T.IDY[:, 0:1], T.IDX[:, 0:1], T.PF[:, 5:6], T.PF[:, 7:8], OP.mult, OP.add))
-    for q in V_THEN[1:]:
-        inj_v(q)
     need("v", "t", tOFF)
-    vOA = vi(v.tensor_copy(T.OFF[:, 8 * BS:256], T.B1[:, 8 * BS:256]))
-    vOB = vi(v.tensor_copy(T.OFF[:, 0:8 * BS], T.B1[:, 0:8 * BS]))
-    vi(v.tensor_copy(T.REP2[:], T.IOG[:]))
-    sB = 0
-    rows = list(S_CHAIN)
-    need("s", "v", vOB)
-    for j in range(BS - 1, -1, -1):
-        need("s", "s", sB)
+    EARLY = ZS + 15
+    vOA = vi(v.tensor_copy(T.OFF[:, 8 * EARLY:256], T.B1[:, 8 * EARLY:256]))
+    vOB = vi(v.tensor_copy(T.OFF[:, 0:8 * EARLY], T.B1[:, 0:8 * EARLY]))
+
+    def end(k):
+        return T.PW[:, 160 * k + 16:160 * k + 144]
+
+    F = [T.PF[:, c:c + 1] for c in range(8, 16)]
+    small = [lambda: s.activation(F[0], T.PI[:, 7:8], FN.Copy, scale=-1.0 / 64),
+             lambda: s.activation(F[1], T.PI[:, 7:8], FN.Identity, bias=160.0, scale=-0.5),
+             lambda: s.activation(F[2], T.PI[:, 6:7], FN.Abs, bias=F[0], scale=0.25),
+             lambda: s.activation(F[3], T.PI[:, 7:8], FN.Identity, bias=T.PF[:, 3:4], scale=0.25),
+             lambda: s.activation(F[5], F[2], FN.Identity, bias=F[3], scale=F[1]),
+             lambda: s.activation(F[6], F[5], FN.Identity, bias=15.0),
+             lambda: s.activation(F[7], T.PI[:, 2:3], FN.Identity, bias=F[6], scale=273.0)]
+    si(small.pop(0)())
+    need("s", "gq", gPW)
+    chain, rows = {BS: 0}, list(S_CHAIN)
+
+    def step_s(j):
+        need("s", "v", vOA if j >= EARLY else vOB)
+        need("s", "s", chain[j + 1])
         win = T.IOTA[:] if j == BS - 1 else blk128(T.WS, j + 1)
-        sB = si(s.activation(blk128(T.WS, j), win.indirect(T.OFF[:, 8 * j:8 * j + 8]), FN.Copy))
-        if rows and j:
+        chain[j] = si(s.activation(blk128(T.WS, j) if j else end(2), win.indirect(T.OFF[:, 8 * j:8 * j + 8]), FN.Copy))
+
+    for j in range(BS - 1, -1, -1):
+        step_s(j)
+        if rows:
             inj_s(rows.pop(0))
+        elif small:
+            need("s", "s", chain[j] - 1)
+            sY = si(small.pop(0)())
     for q in rows + list(S_LAST):
         inj_s(q)
 
@@ -220,163 +253,155 @@ def rank_program(g, core, T, topo):
 
     def step(j):
         first = j in (31, ZS + 15, ZS - 1)
-        win = blk128(T.INJ, row(j)) if first else blk128(T.W, j + 1)
+        win = blk128(T.INJ, row(j)) if first else end(0) if j + 1 == BS else blk128(T.W, j + 1)
+        o = end(0) if j == BS else end(1) if j == ZS + 16 else blk128(T.W, j)
         need("v", *(inj[row(j)] if first else ("v", done[j + 1])))
-        need("v", "v", vOA if j >= BS else vOB)
+        need("v", "v", vOA if j >= EARLY else vOB)
         a = win.indirect(T.OFF[:, 8 * j:8 * j + 8])
         if j in (ZS, ZS + 16):
-            done[j] = vi(v.tensor_copy(blk128(T.W, j), a))
+            done[j] = vi(v.tensor_copy(o, a))
         else:
-            need("v", *inj[row(j - 1)])
-            done[j] = vi(v.tensor_tensor(blk128(T.W, j), a, blk128(T.INJ, row(j - 1)), OP.add))
+            need("v", *inj[row(j - 1) if j else "joined"])
+            done[j] = vi(v.tensor_tensor(o, a, blk128(T.INJ, row(j - 1)) if j else T.WB[:], OP.add))
 
+    need("v", "gq", gPW)
     for n in range(16 - ZS):
-        if rank == 0 and n == 15 - ZS:
-            need("v", "s", sB)
-            vi(v.memset(T.U[:, 53:54], 0))
-            vU = vi(v.tensor_copy(T.U[:, 0:1], T.WS[:, 0:1]))
         step(ZS + 15 - n)
         step(31 - n)
-    later = [j for n in range(ZS) for j in (ZS - 1 - n, BS - 1 - n)]
-    gi(g.affine_select(T.SEL[:, 0:48], T.ONES[:, 0:48], [[-2000, 2], [-16, 8], [1000, 3]], OP.is_equal, 0.0, 0, 1))
-    gi(g.affine_select(T.SEL[:, 48:72], T.ONES[:, 0:24], [[-16, 8], [1000, 3]], OP.is_equal, 0.0, -1015, 1))
-    n2 = gi(g.affine_select(T.SC[:], T.ONES[:], [[0, 128]], OP.is_gt, 1.0 / 128, 0, 0))
-    iota(T.IOR[:], [[2, 4]], 0)
-    need("g", "gq", n2)
-    n2 = gi(g.affine_select(T.BLKA[:], T.SC[:], [[-16, 8], [0, 16]], OP.is_ge, 0.0, 0, 1))
-    gi(g.affine_select(T.ID[:], T.ONES[:], [[1, 128]], OP.is_equal, 0.0, 0, -1))
-    need("g", "gq", n2)
-    gC = gi(g.affine_select(T.BLK[:], T.BLKA[:], [[16, 8], [0, 16]], OP.is_ge, 0.0, 15, -1))
+    sB = chain[0]
+    need("v", "s", sY)
+    vTL = vi(v.tensor_copy(T.TL[:, 0::2], T.PF[:, 14:16]))
+    gi(g.affine_select(T.SC[:], T.ONES[:], [[0, 128]], OP.is_gt, 1.0 / 128, 0, 0))
+    iota(T.MT0[:], [[128, 4], [0, 8]], 128 * 129)
+    gIO = iota(T.IO0[:], [[-32, 2], [16, 4]], 64 * rank + 32)
+    gC = iota(T.IOR[:], [[2, 4]], 0)
     need("g", "v", vID)
-
-    n3 = iota(T.MT0[:], [[128, 4], [0, 8]], 128 * 129)
-    gIO = iota(T.IO0[:], [[-67, 2], [16, 4]], 64 * rank + 72)
-    need("g", "gq", n3)
-    n3 = gi(g.affine_select(T.MT1[:], T.MT0[:], [[0, 4], [-16, 8]], OP.is_ge, 1e6, 0, 1))
     need("g", "ldem", 32)
     for h in range(2):
         g.indirect_dma_start(T.AE[:, 256 * h:256 * h + 256], None, T.emd[:],
                              IndirectOffsetOnAxis(ap=T.IDY[:, h:h + 1], axis=0), bounds_check=511).then_inc(S.ge, 16)
-    if rank == 0:
-        need("v", "v", done[BS])
-        n = vi(v.tensor_copy(T.U[:, 18:34], blk128(T.W, BS).indirect(T.U[:, 0:1])))
-        step(later.pop(0))
-        need("v", "v", n)
-        n = vi(v.tensor_copy(T.U[:, 37:53], blk128(T.W, ZS + 16).indirect(T.U[:, 18:19])))
-        need("g", "v", n)
-        for part in parts(topo, T, rank):
-            send(part, "u0", T.U[:, 52:54], [T.UR[:, 0:2]] * len(part))
-    o = T.B2[:, 0:24]
-    need("t", "gq", gC)
-    need("t", "v", done[BS])
-    t.matmul(o, blk128(T.W, BS), T.SEL[:, 48:72], True, False)
-    need("t", "s", sB)
-    t.matmul(o, blk128(T.WS, 0), T.SEL[:, 0:24], False, False)
-    need("t", "v", done[ZS + 16])
-    tX = ti(t.matmul(o, blk128(T.W, ZS + 16), T.SEL[:, 24:48], False, True))
-    step(later.pop(0))
-    step(later.pop(0))
-    need("v", "gq", gC)
-    vRP = vi(v.tensor_scalar(T.REP[:], T.IOR[:], T.PF[:, 2:3], None, OP.add))
-    wide = 24 * (rank - 1)
-    if rank > 1:
-        vXL = vi(v.tensor_scalar(T.XL[:], T.IOG[:, 0:8], T.PF[:, 8:9], wide - 1.0, OP.add, OP.min))
-    need("v", "t", tX)
-    vX = vi(v.tensor_copy(T.XS[:], o))
+    def turn(k):
+        vi(v.transpose(T.TT[:, 288 * k:288 * k + 128], end(k)))
+        return vi(v.transpose(T.TT[:, 288 * k + 128:288 * k + 288], T.PW[:, 160 * k:160 * k + 160]))
+
+    later = [j for n in range(ZS) for j in (ZS - 1 - n, BS - 1 - n)]
+    need("v", "v", done[BS])
+    n = turn(0)
     if rank and sends:
-        need("g", "v", vX)
-        for part in parts(topo, T, rank):
-            send(part, "arr", T.XS[:], [T.XR[:, 24 * rank - 24:24 * rank]] * len(part))
+        need("v", "v", done[ZS + 16])
+        n = turn(1)
     step(later.pop(0))
-    need("v", "v", vX)
-    for k in (1, 0):
-        n = vi(v.tensor_tensor(blk128(T.XM, k), T.XS[:].indirect(T.REP2[:, 8 * k:8 * k + 8]), T.MASKI[:], OP.mult))
-        need("t", "v", n)
-        m = t.matmul(T.B3[:, 8 * k:8 * k + 8], blk128(T.XM, k), T.BLK[:, 0::16], True, True)
-    tL = ti(m)
-    step(later.pop(0))
-    step(later.pop(0))
-    need("v", "t", tL)
-    vL = vi(v.tensor_copy(T.LS[:], T.B3[:, 0:16]))
-    if rank > 1 and sends:
+    need("v", "v", max(n, vTL))
+    if rank and sends:
+        n = vi(v.tensor_copy(T.LS[:, 0:16], T.TT[:, 0:576].indirect(T.TL[:, 2:3])))
+        need("g", "v", n)
+        send(after(T, rank), "arr%d" % rank, T.LS[:, 0:16], T.LR[:, 24 * rank - 24:24 * rank - 8])
+        need("v", "s", sB)
+        m = turn(2)
+    else:
+        n = vi(v.tensor_copy(T.LS[:, 0:16], T.TT[:, 0:288].indirect(T.TL[:, 0:1])))
+        step(later.pop(0))
+        need("v", "s", sB)
+    need("s", "v", max(n, done[ZS + 16]))
+    sWA = si(s.activation(T.WA[:], end(1).indirect(T.LS[:, 0:8]), FN.Copy))
+    if rank == 0:
+        n = vi(v.tensor_copy(T.U[:, 0:2], T.PW[:, 336:338]))
+        m = turn(2)
+        need("v", "s", sWA)
+        need("v", "v", n)
+        n = vi(v.tensor_copy(T.U[:, 16:32], T.WA[:].indirect(T.U[:, 0:1])))
+        need("g", "v", n)
+        send(after(T, rank), "u0", T.U[:, 16:18], T.UR[:, 0:2])
+    else:
+        if not sends:
+            m = turn(2)
+        step(later.pop(0))
+    need("v", "v", m)
+    vL = vi(v.tensor_copy(T.LS[:, 16:32], T.TT[:, 576:864].indirect(T.TL[:, 0:1])))
+    if rank and sends:
         need("g", "v", vL)
-        for part in parts(topo, T, rank):
-            send(part, "lst", T.LS[:], [T.LR[:, 16 * rank - 32:16 * rank - 16]] * len(part))
-    need("g", "gq", n3)
+        send(after(T, rank), "lst%d" % rank, T.LS[:, 16:24], T.LR[:, 24 * rank - 8:24 * rank])
+    need("g", "gq", gC)
+    n2 = gi(g.affine_select(T.BLKA[:], T.SC[:], [[-16, 8], [0, 16]], OP.is_ge, 0.0, 0, 1))
+    gi(g.affine_select(T.MT1[:], T.MT0[:], [[0, 4], [-16, 8]], OP.is_ge, 1e6, 0, 1))
+    need("g", "gq", n2)
+    n2 = gi(g.affine_select(T.BLK[:], T.BLKA[:], [[16, 8], [0, 16]], OP.is_ge, 0.0, 15, -1))
+    iota(T.CN[:], [[0, 2]], -16512)
+    need("g", "gq", n2)
     gi(g.affine_select(T.TRI[:], T.BLK[:], [[1, 128]], OP.is_gt, 0.0, 0, -1))
     gi(g.affine_select(T.BH[:], T.BLK[:], [[0, 8], [1, 16]], OP.is_ge, 0.0, -ZS - 1, 0))
-    gi(g.affine_select(T.BL[:], T.BLK[:], [[16, 8], [0, 16]], OP.is_ge, 0.0, ZS, -1))
-    gT = iota(T.CN[:], [[16512, 2], [0, 2]], -16512)
+    gT = gi(g.affine_select(T.BL[:], T.BLK[:], [[16, 8], [0, 16]], OP.is_ge, 0.0, ZS, -1))
     gi(g.affine_select(T.MT[:], T.MT1[:], [[0, 4], [16, 8]], OP.is_ge, 1e6, 15, -1))
     iota(T.IOTAM[:], [[-32, 2], [1, 35]], -3)
     iota(T.IOTAZ[:], [[1, 100]], -3)
-    iota(T.MS[:, 0:5], [[0, 5]], 0)
+    if not sends:
+        gi(g.affine_select(T.ID[:], T.ONES[:], [[1, 128]], OP.is_equal, 0.0, 0, -1))
     if rank == 0:
-        iota(T.WP[:, 0:72], [[0, 72]], 0)
+        iota(T.WP[:, 0:32], [[0, 32]], 0)
     gALL = cnt["gq"]
-    for j in later:
-        step(j)
-    need("s", "s", inj[1][1])
-    sVZ = si(s.activation(T.VBZ[:], T.INJ[:, 0:1024], FN.Copy, scale=0.0))
-    need("s", "v", vL)
-    n = si(s.activation(T.WA[:], blk128(T.W, ZS + 16).indirect(T.LS[:, 8:16]), FN.Copy))
-    sDB = si(s.activation(T.DIAGB[:], T.MASKQ[:], FN.Copy, scale=16448.5))
-    need("s", "s", n)
-    sWB = si(s.activation(T.WB[:], T.WA[:].indirect(T.LS[:, 0:8]), FN.Copy, scale=T.PF[:, 6:7]))
     need("s", "gq", gIO)
     sIO = si(s.activation(T.IO[:], T.IO0[:], FN.Identity, bias=T.PF[:, 0:1]))
+    sDB = si(s.activation(T.DIAGB[:], T.MASKQ[:], FN.Copy, scale=16448.5))
+    need("s", "s", sWA)
+    need("s", "v", vL)
+    sWB = si(s.activation(T.WB[:], T.WA[:].indirect(T.LS[:, 16:24]), FN.Copy, scale=T.PF[:, 6:7]))
+    sVZ = si(s.activation(T.VBZ[:, 0:512], T.WS[:, 128:640], FN.Copy, scale=0.0))
     ucol, L, vU = T.UR[:, 0:1], 0, 0
     if rank == 0:
         vU = vi(v.memset(T.UR[:], 0))
     made = {}
-    if rank > 1:
-        for q in "vs":
-            need(q, "v", vXL)
-            need(q, "arr", from_parts(range(1, rank)))
-        vQ = vi(v.tensor_copy(T.XQ[:, 0:64], T.XR[:, 0:wide].indirect(T.XL[:, 0:4])))
-        sQ = si(s.activation(T.XQ[:, 64:128], T.XR[:, 0:wide].indirect(T.XL[:, 4:8]), FN.Copy))
-        need("t", "v", vQ)
-        need("t", "s", sQ)
-        tW = ti(t.matmul(T.B4[:, 0:128], T.XQ[:], T.ID[:], True, True))
-    need("v", "s", sWB)
-    need("v", "v", done[0])
-    vJ = vi(v.tensor_tensor(T.WZ[:], T.WB[:], blk128(T.W, 0), OP.add))
-    if rank > 1:
-        need("v", "t", tW)
-        vU = vW = vi(v.tensor_copy(T.WIN[:], T.B4[:, 0:128]))
 
     def compose(q, r, k):
-        need(q, "v", vW)
-        need(q, "lst", from_parts(range(2, rank)))
-        if k == 0:
-            need(q, q, made[r])
-        win = (T.WIN[:] if k else blk128(T.CW, 2 * r - 3)).indirect(T.LR[:, 16 * r - 32 + 8 * k:16 * r - 24 + 8 * k])
-        o = blk128(T.CW, 2 * r - 4 + k)
-        made[r] = vi(v.tensor_copy(o, win)) if q == "v" else si(s.activation(o, win, FN.Copy))
+        need(q, ("arr%d" if k < 2 else "lst%d") % r, from_parts([r]))
+        if k:
+            need(q, *made[r, k - 1])
+        a = 24 * r - (16, 24, 8)[k]
+        o, win = blk128(T.CW, 3 * r - 3 + k), (blk128(T.CW, 3 * r - 4 + k) if k else T.IOTA[:]).indirect(T.LR[:, a:a + 8])
+        made[r, k] = (q, vi(v.tensor_copy(o, win)) if q == "v" else si(s.activation(o, win, FN.Copy)))
 
-    for k in (1, 0):
-        for r in range(2, min(rank, 4)):
-            compose("s", r, k)
+    inj["joined"] = ("s", sWB)
+    fill = [lambda j=j: step(j) for j in later if j != ZS]
+    while len(fill) > V_LEFT:
+        fill.pop(0)()
+    need("v", "gq", gC)
+    vRP = vi(v.tensor_scalar(T.REP[:], T.IOR[:], T.PF[:, 2:3], None, OP.add))
+    for q, r, k in MAKES:
+        if r < rank:
+            compose(q, r, k)
+        elif q == "v" and fill:
+            fill.pop(0)()
     need("t", "gq", gT)
-    t.matmul(T.B6[:, 0:3], T.TRI[:], T.CN[:, 0:3], True, False)
-    for col, mat in ((0, T.BH), (1, T.BL), (2, T.BLK), (2, T.BLK)):
+    t.matmul(T.B6[:, 0:2], T.TRI[:], T.CN[:], True, False)
+    for col, mat in enumerate((T.BH, T.BL)):
         t.matmul(T.B6[:, col:col + 1], mat[:], T.CN[:, 0:1], False, False)
+        t.matmul(T.B4[:, 0:1], T.BLK[:], T.CN[:, 0:1], col == 0, False)
     if rank:
         need("v", "u0", from_parts([0]))
-    hops = [(T.WIN[:], k, 0) for k in range(3)] + [(blk128(T.CW, 2 * r - 4), 3 * r - 1, r) for r in range(2, rank)]
-    for k, (win, valid, r) in enumerate(hops if rank > 1 else []):
-        a = 18 * k + L % 2
+    last = (T.IOTA[:], ucol, 0)
+    for r in range(1, rank):
+        last = (blk128(T.CW, 3 * r - 1), ucol, max(vU, made[r, 2][1] * (made[r, 2][0] == "v")))
         need("v", "v", vU)
-        if r:
-            need("v", "sv"[r // 4], made[r])
-        vU = vi(v.tensor_copy(T.U[:, a:a + 16], win.indirect(ucol)))
-        ucol, L = T.U[:, a + L:a + L + 1], valid
-        if rank > 4 and k < 2:
-            compose("v", 4, 1 - k)
-    need("v", "v", max(vU, vJ, done[ZS]))
+        need("v", *made[r, 2])
+        vU = vi(v.tensor_copy(T.U[:, 16 * r:16 * r + 16], last[0].indirect(ucol)))
+        ucol = T.U[:, 16 * r:16 * r + 1]
+        if fill:
+            fill.pop(0)()
+    while fill:
+        fill.pop(0)()
+    need("s", "v", done[ZS + 1])
+    sW = si(s.activation(blk128(T.W, ZS), blk128(T.W, ZS + 1).indirect(T.OFF[:, 8 * ZS:8 * ZS + 8]), FN.Copy))
+    if rank:
+        need("s", "u0", from_parts([0]))
+        need("s", "v", last[2])
+        need("s", "s", sW - 1)
+        sU = si(s.activation(T.UF[:], last[0].indirect(last[1]), FN.Copy, scale=T.MASKQ[:, 0:1]))
+        need("v", "s", sU)
+    sVZ = si(s.activation(T.VBZ[:, 512:1024], T.WS[:, 128:640], FN.Copy, scale=0.0))
+    need("v", "v", max(vU, done[0]))
     a, b = L % 2, ZS % 2
     lists = (T.SA[:, a + L:a + L + 1], T.S0[:, b + ZS:b + ZS + 1])
-    n = vi(v.tensor_copy(T.SA[:, a:a + 16], T.WZ[:].indirect(ucol)))
+    n = vi(v.tensor_scalar(T.SA[:, a:a + 16], blk128(T.W, 0).indirect(ucol), T.UF[:, 0:1] if rank else 0.0, None, OP.add))
+    need("v", "s", sW)
     need("v", "v", n)
     vS = vi(v.tensor_copy(T.S0[:, b:b + 16], blk128(T.W, ZS).indirect(lists[0])))
     need("v", "s", sDB)
@@ -384,63 +409,70 @@ def rank_program(g, core, T, topo):
     vC, vE = {}, {}
     for h in range(2):
         need("v", "v", vS if h else 0)
-        vC[h] = vi(v.tensor_tensor(T.CM[:, 16 * h:16 * h + 16], blk128(T.AE, 2 * h + 1).indirect(lists[h]), T.DIAGB[:], OP.add))
         vE[h] = vi(v.tensor_tensor(T.EM[:, 16 * h:16 * h + 16], blk128(T.AE, 2 * h).indirect(lists[h]), T.MASKQ[:], OP.mult))
+        vC[h] = vi(v.tensor_tensor(T.CM[:, 16 * h:16 * h + 16], blk128(T.AE, 2 * h + 1).indirect(lists[h]), T.DIAGB[:], OP.add))
     for h in range(2):
-        need("v", "v", vC[h])
-        vC[h] = vi(v.tensor_reduce(T.CS[:, h:h + 1], T.CM[:, 16 * h:16 * h + 16], AxisListType.X, OP.max))
         need("v", "v", vE[h])
         vR = vi(v.tensor_reduce(T.E2[:, h:h + 1], T.EM[:, 16 * h:16 * h + 16], AxisListType.X, OP.max))
+        need("v", "v", vC[h])
+        vC[h] = vi(v.tensor_reduce(T.CS[:, h:h + 1], T.CM[:, 16 * h:16 * h + 16], AxisListType.X, OP.max))
     for h in range(2):
         need("t", "v", vC[h])
         t.matmul(T.B6[:, h:h + 1], T.TRI[:], T.CS[:, h:h + 1], False, False)
-        t.matmul(T.B6[:, 1 - h:2 - h], (T.BL, T.BH)[h][:], T.CS[:, h:h + 1], False, False)
-        m = t.matmul(T.B6[:, 2:3], T.BLK[:], T.CS[:, h:h + 1], False, h == 1)
+        m = t.matmul(T.B6[:, 1 - h:2 - h], (T.BL, T.BH)[h][:], T.CS[:, h:h + 1], False, h == 1)
     tB = ti(m)
-    need("v", "gq", gALL)
     for h in range(2):
-        need("v", "v", vC[h])
-        vi(v.tensor_scalar(T.GTB[:, 32 * h:32 * h + 32], T.MT[:], T.CS[:, h:h + 1], None, OP.is_lt))
+        m = t.matmul(T.B4[:, 0:1], T.BLK[:], T.CS[:, h:h + 1], False, h == 1)
+    tN = ti(m)
+    need("v", "gq", gALL)
+    need("v", "v", vC[0])
+    vi(v.tensor_scalar(T.GTB[:, 0:32], T.MT[:], T.CS[:, 0:1], None, OP.is_lt))
     need("v", "v", vR)
     vi(v.tensor_scalar(T.D[:, 0::4], T.E2[:], 63, None, OP.bitwise_and))
     for m in range(1, 4):
         vD = vi(v.tensor_scalar(T.D[:, m::4], T.E2[:], 6 * m, 63, OP.logical_shift_right, OP.bitwise_and))
+    need("v", "v", vC[1])
+    vG = vi(v.tensor_scalar(T.GTB[:, 32:64], T.MT[:], T.CS[:, 1:2], None, OP.is_lt))
     need("v", "t", tB)
-    wide, head = (67, 35) if sends else (35, 38)
+    wide = 67 if sends else 32
     for h in range(2):
-        vO = vi(v.tensor_scalar(T.OHM[:, 70 * h:70 * h + head], T.IOTAM[:, 0:head], T.B6[:, h:h + 1], None, OP.is_equal))
+        vO = vi(v.tensor_scalar(T.OHM[:, 70 * h:70 * h + 35], T.IOTAM[:, 0:35], T.B6[:, h:h + 1], None, OP.is_equal))
+        need("v", "v", vG if h else max(vD, vRP))
+        need("v", "s", sVZ)
+        vO = vi(v.tensor_tensor(T.VBZ[:, 512 * h:512 * h + 512:16], T.D[:].indirect(T.REP[:, 2 * h:2 * h + 2]),
+                                T.GTB[:, 32 * h:32 * h + 32], OP.mult))
         if sends:
-            vO = vi(v.tensor_scalar(T.OHM[:, 70 * h + 35:70 * h + 70], T.IOTAM[:, 35:70], T.B6[:, 2:3], T.B6[:, h:h + 1],
+            need("v", "t", tN)
+            vO = vi(v.tensor_scalar(T.OHM[:, 70 * h + 35:70 * h + 70], T.IOTAM[:, 35:70], T.B4[:, 0:1], T.B6[:, h:h + 1],
                                     OP.add, OP.is_equal))
-        if h == 0:
-            need("v", "v", max(vD, vRP))
-            need("v", "s", sVZ)
-            vO = vi(v.tensor_tensor(T.VBZ[:, 0::16], T.D[:].indirect(T.REP[:]), T.GTB[:], OP.mult))
+        if sends and h == 0:
+            vN = vi(v.tensor_copy(T.CNT[:], T.B4[:, 0:1]))
+            need("g", "v", vN)
+            send(after(T, rank)[::-1], "cn", T.CNT[:], T.MR[:, rank:rank + 1], "rest")
         need("t", "v", vO)
         for m in range(4):
             ins = t.matmul(T.B5[:, 0:wide], blk128(T.VBZ, 4 * h + m), T.OHM[:, 70 * h + 3 - m:70 * h + 3 - m + wide],
                            h + m == 0, h + m == 4)
     tM = ti(ins)
-    vN = vi(v.tensor_copy(T.CNT[:], T.B6[:, 2:3]))
-    if sends:
-        need("g", "v", vN)
-        for part in parts(topo, T, rank)[::-1]:
-            send(part, "cn", T.CNT[:], [T.MR[:, rank:rank + 1]] * len(part))
+    if not sends:
+        need("v", "t", tN)
+        vN = vi(v.tensor_copy(T.CNT[:], T.B4[:, 0:1]))
     for h in range(2):
         vO = vi(v.tensor_scalar(T.OHZ[:, 100 * h:100 * h + 100], T.IOTAZ[:], T.B6[:, h:h + 1], None, OP.is_equal))
     need("v", "s", sIO)
     need("v", "v", vN)
     if sends:
+        vi(v.tensor_scalar(T.GAP[:], T.CNT[:], -1.0, 96.0, OP.mult, OP.add))
         n = vi(v.tensor_scalar(T.IO[:, 4:8], T.IO[:, 4:8], T.CNT[:], None, OP.subtract))
     else:
         n = vO = vi(v.tensor_scalar(T.GE[:], T.IOTA[:, 0:96], T.CNT[:], -1.0, OP.is_ge, OP.mult))
     need("v", "t", tM)
-    vM = vi(v.tensor_copy(T.MS[:, 5:5 + wide], T.B5[:, 0:wide]))
+    vM = vi(v.tensor_copy(T.MS[:, 0:wide], T.B5[:, 0:wide]))
     need("g", "gq", gALL)
     need("g", "v", vM)
-    to = beside(T, rank)
-    send([T.cores[r] for r in to], "z%d" % rank, T.MS[:, 0:5 + wide],
-         [(T.WP if r > rank else T.WN)[:, 0:5 + wide] for r in to])
+    g.remote_dma_fused([transfer(to, engines, "z", *((T.MS[:, 35:67], T.WP[:, 0:32]) if to[0] > rank else
+                                                     (T.MS[:, 0:32], T.WP[:, 128:160])))
+                        for to, engines in deal(topo, T, rank, beside(T, rank), "both")], local_sem=S.lsf)
     g.wait_ge(S.lsf, cnt["lsf"])
     need("t", "v", vO)
     for k in range(8):
@@ -450,21 +482,24 @@ def rank_program(g, core, T, topo):
         ins = t.matmul(T.B7[:, 0:96], T.ID[:], T.GE[:], False, True)
     tZ = ti(ins)
     need("s", "t", tZ)
-    sZ = si(s.activation(T.WP[:, 72:168], T.B7[:, 0:96], FN.Copy))
+    sZ = si(s.activation(T.WP[:, 32:128], T.B7[:, 0:96], FN.Copy))
     if rank:
-        need("v", "cn", from_parts(range(rank)))
+        need("v", "cn", from_parts(range(rank), after, "rest"))
         n = vi(v.tensor_reduce(T.SUM[:], T.MR[:, 0:rank], AxisListType.X, OP.add))
     need("v", "v", n)
-    n = vi(v.tensor_scalar(T.YL[:], T.IO[:], T.SUM[:] if rank else 0.0, 4.0, OP.subtract, OP.max))
+    before = T.SUM[:] if rank else 0.0
+    if sends:
+        vi(v.tensor_scalar(T.IP[:, 0:4], T.IO[:, 0:4], before, None, OP.subtract))
+        n = vi(v.tensor_scalar(T.IP[:, 4:8], T.IO[:, 4:8], before, 0.0, OP.subtract, OP.is_ge))
+        need("v", "v", n)
+        for c in range(4):
+            n = vi(v.tensor_scalar(T.YL[:, c:c + 1], T.IP[:, 4 + c:5 + c], T.GAP[:], T.IP[:, c:c + 1], OP.mult, OP.add))
+    else:
+        n = vi(v.tensor_scalar(T.YL[:], T.IO[:, 0:4], before, None, OP.subtract))
     need("v", "v", n)
     need("v", "s", sZ)
-    if rank:
-        heard("v", rank - 1)
-    n = vi(v.tensor_copy((T.Y1 if sends else T.YS)[:], T.WP[:].indirect(T.YL[:, 0:4])))
-    if sends:
-        need("v", "v", n)
-        heard("v", rank + 1)
-        n = vi(v.tensor_tensor(T.YS[:], T.WN[:, 0:40].indirect(T.YL[:, 4:8]), T.Y1[:], OP.add))
+    need("v", "z", from_parts(beside(T, rank), beside, "both"))
+    n = vi(v.tensor_copy(T.YS[:], T.WP[:, 0:160 if sends else 128].indirect(T.YL[:])))
     need("y", "v", n)
     y.dma_start(T.y[:], T.YS[0::16, :]).then_inc(S.st, 16)
     y.wait_ge(S.st, 16)

from concourse.mybir import dt, AluOpType, AxisListType, ActivationFunctionType
from concourse.bass import IndirectOffsetOnAxis, DstId, RemoteDMATransfer

SCRATCH = {"emd": ("dram", [512, 256], "int32")}
for _t, _l in (
    ("int32", "TN:32,16 TS:32,16 SY:128 IDX:4 IDY:2 AE:512 EM:32 E2:2 D:8 P:1 PI:8 P16:16 Q16:16"),
    ("bfloat16", "TBLK:32,32 SYM:128 O:128 INJ:2048 W:4096 WS:1536 PW:480 TT:864 "
                 "CM:32 CS:2 CN:2 GTB:64 VBZ:1024 OHM:140 OHZ:200 MS:72 WP:160 ONES:128 SC:128 L2:128 "
                 "ID:128 BLKA:128 BLK:128 TRI:128 BH:128 BL:128 IOTA:128 IOTAM:70 IOTAZ:100 GE:96 "
                 "WA:128 WB:128 CW:1536"),
    ("uint16", "OFF:256 UR:8 U:128 S0:18 SA:18 REP:4 YL:4 TL:4 LS:32 LR:96"),
    ("float32", "UF:16 IP:8 GAP:1 YS:64 PF:16 PX:1 MASKQ:16 DIAGB:16 IOR:4 IO0:8 IO:8 MT0:32 MT1:32 MT:32 "
                "CNT:1 MR:8 SUM:1"),
):
    for _b in _l.split():
        _n, _d = _b.split(":")
        SCRATCH[_n] = ("sbuf", [128] + [int(_x) for _x in _d.split(",")], _t)
for _b in range(8):
    SCRATCH["B%d" % _b] = ("psum", [128, 512], "float32")
SEMAPHORES = ["ldsy", "ldn0", "ldn1", "ldn2", "ldn3", "ldem", "ldidx", "v", "t", "s", "gq", "ge",
              "arr1", "arr2", "arr3", "arr4", "lst1", "lst2", "lst3", "lst4", "u0", "cn",
              "z", "lsf", "st", "ib"]
OP = AluOpType
FN = ActivationFunctionType
ZS = 6
BS = 12
S_FIRST, V_FIRST, S_THEN, V_THEN, S_CHAIN, S_LAST = (0, 15), (14,), (12, 11, 10), (13, 9, 8), (), ()
BY_DMA = 7
MAKES = (("s", 1, 0), ("s", 2, 0), ("s", 1, 1), ("s", 2, 1), ("v", 3, 0), ("v", 4, 0), ("s", 3, 1), ("s", 4, 1),
         ("v", 1, 2), ("v", 2, 2), ("s", 3, 2), ("s", 4, 2))
V_LEFT = 2


def deal(topo, T, r, to, how="out"):
    me = T.cores[r]
    away = [x for x in range(len(T.cores)) if topo.chip(T.cores[x]) != topo.chip(me)]
    mate = [x for x in range(len(T.cores)) if x not in away and x != r][0]
    out = [e for e in topo.engines(me, T.cores[away[0]]) if all(e in topo.engines(me, T.cores[x]) for x in away)]
    rest = [e for e in topo.engines(me, T.cores[mate]) if e not in out]
    first = [x for x in to if x in away] or {"out": to, "rest": [], "both": to[:1]}[how]
    return [p for p in ((first, out), ([x for x in to if x not in first], rest)) if p[0]]


def after(T, r):
    return list(range(len(T.cores) - 1, r, -1))


def beside(T, r):
    return [x for x in (r + 1, r - 1) if 0 <= x < len(T.cores)]


def dst_id(topo, d):
    rid, pid, _ = topo.addr(d)
    return DstId(rid=rid, pnc=pid)


def rank_program(g, core, T, topo):
    rank = T.rank_of(core)
    if rank is None:
        return
    v, t, s, y = g.vector, g.tensor, g.scalar, g.sync
    S = T.sem
    N = len(T.cores)
    sends = rank < N - 1
    cnt = {"v": 0, "t": 0, "s": 0, "gq": 0, "lsf": 0}
    seen = {}
    queues = {"v": v, "t": t, "s": s, "y": y, "g": g}

    def inc(key, ins):
        ins.then_inc(S[key], 1)
        cnt[key] += 1
        return cnt[key]

    def vi(ins):
        return inc("v", ins)

    def ti(ins):
        return inc("t", ins)

    def si(ins):
        return inc("s", ins)

    def gi(ins):
        return inc("gq", ins)

    def need(q, key, n):
        if n and seen.get((q, key), 0) < n:
            queues[q].wait_ge(S[key], n)
            seen[(q, key)] = n

    def transfer(ranks, engines, sem, src, dst):
        cnt["lsf"] += len(engines)
        return RemoteDMATransfer(dst_ids=[dst_id(topo, T.cores[x]) for x in ranks], dma_engine_mask=sum(1 << e for e in engines),
                                 remote_sem=S[sem], srcs=[src], dsts=[dst] * len(ranks), alu_op=0)

    def send(to, sem, src, dst, how="out"):
        for ranks, engines in deal(topo, T, rank, to, how):
            g.remote_dma_fused([transfer(ranks, engines, sem, src, dst)], local_sem=S.lsf)

    def from_parts(senders, to=after, how="out"):
        return sum(len(engines) for r in senders for ranks, engines in deal(topo, T, r, to(T, r), how) if rank in ranks)

    def iota(out, pattern, base, cm=0):
        return gi(g.iota(out, pattern, base, cm, allow_small_or_imprecise_dtypes=True))

    def blk128(buf, k):
        return buf[:, 128 * k:128 * k + 128]

    y.dma_start(T.SY[0:1, :], T.sy[0::2, :]).then_inc(S.ldsy, 16)
    s.dma_start(T.SY[1:2, :], T.sy[1::2, :]).then_inc(S.ldsy, 16)
    for i in range(4):
        (y, s)[i % 2].dma_start(T.TN[:, 8 * i:8 * i + 8, :], T.nx[2 * i:2 * i + 2, :]).then_inc(S["ldn%d" % i], 16)
    for h, j in enumerate((0, ZS + 1, 16)):
        y.dma_start(T.IDX[:, h:h + 1], T.sy[:, j:j + 16]).then_inc(S.ldidx, 16)

    gP16 = gi(g.iota(T.P16[:], [[-1, 16]], 16, 1))
    gP = gi(g.iota(T.P[:], [[1, 1]], 0, 4))
    gI = iota(T.IOTA[:], [[1, 128]], 0)
    v_ones = vi(v.memset(T.ONES[:], 1.0))
    need("g", "v", v_ones)
    gL2 = gi(g.affine_select(T.L2[0:2, :], T.ONES[0:2, :], [[1, 2], [0, 64]], OP.is_equal, 0.0, 0, -1))
    y.wait_ge(S.ldn0, 16)
    y.dma_start(T.emd[:, 0:128], T.em[:]).then_inc(S.ldem, 16)
    y.dma_start(T.emd[:, 128:256], T.nx[:]).then_inc(S.ldem, 16)
    gPW = iota(T.PW[:], [[0, 480]], 0)
    inj = {}
    need("y", "gq", iota(T.INJ[:, 128:128 + 128 * BY_DMA], [[0, 128 * BY_DMA]], 0))
    for q in range(BY_DMA, 0, -1):
        y.dma_start(T.INJ[q::16, 128 * q:128 * q + 128], T.IOTA[q::16, :]).then_inc(S.ib, 16)
        inj[q] = ("ib", 16 * BY_DMA)
    vi(v.memset(T.TBLK[:], 0.0))
    need("v", "gq", gP)
    vi(v.tensor_scalar(T.PI[:, 3:4], T.P[:], 2, 63, OP.logical_shift_right, OP.bitwise_and))
    n = vi(v.tensor_scalar(T.Q16[:], T.P16[:], 15, None, OP.bitwise_and))
    vi(v.tensor_scalar(T.PI[:, 0:1], T.P[:], 2, 15, OP.logical_shift_right, OP.bitwise_and))
    vi(v.tensor_scalar(T.PI[:, 1:2], T.P[:], 448, None, OP.bitwise_and))
    vP = vi(v.tensor_scalar(T.PI[:, 2:3], T.P[:], 5, 1, OP.logical_shift_right, OP.bitwise_and))
    need("v", "v", n)
    vMQ = vi(v.tensor_scalar(T.MASKQ[:], T.Q16[:], 0.0, None, OP.is_equal))
    vPX = vi(v.tensor_copy(T.PX[:], T.PI[:, 3:4]))
    for c, bits in ((5, 24), (6, 4), (7, 64)):
        vi(v.tensor_scalar(T.PI[:, c:c + 1], T.P[:], bits, None, OP.bitwise_and))

    def inj_v(q):
        need("v", "gq", gI)
        need("v", "v", vMQ)
        inj[q] = ("v", vi(v.tensor_scalar(blk128(T.INJ, q), T.IOTA[:], T.MASKQ[:, q:q + 1], None, OP.mult)))

    def inj_s(q):
        need("s", "gq", gI)
        need("s", "v", vMQ)
        inj[q] = ("s", si(s.activation(blk128(T.INJ, q), T.IOTA[:], FN.Copy, scale=T.MASKQ[:, q:q + 1])))

    for q in S_FIRST:
        inj_s(q)
    need("v", "ldsy", 32)
    vS0 = vi(v.tensor_copy(T.SYM[0:2, :], T.SY[0:2, :]))
    for q in V_FIRST:
        inj_v(q)
    need("t", "gq", gL2)
    need("t", "v", vS0)
    tSO = ti(t.matmul(T.B0[:, 0:128], T.L2[0:2, :], T.SYM[0:2, :], True, True))
    blk, vTS = {}, {}

    def states(i):
        r8 = slice(8 * i, 8 * i + 8)
        need("v", "ldn%d" % i, 16)
        vTS[i] = vi(v.tensor_scalar(T.TS[:, r8, :], T.TN[:, r8, :], 127, None, OP.bitwise_and))

    def blocks(i):
        r8 = slice(8 * i, 8 * i + 8)
        need("v", "v", vTS[i])
        need("s", "v", vTS[i])
        n = vi(v.tensor_copy(T.TBLK[0:64, r8, 0:16], T.TS[0:64, r8, :]))
        if i == 3:
            n = vi(v.tensor_copy(T.TBLK[64:128, 24:27, 16:32], T.TS[64:128, 24:27, :]))
            r8 = slice(27, 32)
        blk[i] = (n, si(s.activation(T.TBLK[64:128, r8, 16:32], T.TS[64:128, r8, :], FN.Copy)))

    states(0)
    states(1)
    blocks(0)
    need("v", "t", tSO)
    need("v", "v", vPX)
    vO = vi(v.tensor_scalar(T.O[:], T.B0[:, 0:128], T.PX[:], None, OP.is_equal))
    states(2)
    blocks(1)
    states(3)
    blocks(2)
    blocks(3)
    for i in range(4):
        need("t", "v", max(vO, blk[i][0]))
        need("t", "s", blk[i][1])
        for c in range(8):
            m = t.matmul(T.B1[32 * i:32 * i + 32, c:256:8], T.TBLK[:, 8 * i + c, :], T.O[:, 32 * i:32 * i + 32], True, True)
    tOFF = ti(m)
    for q in S_THEN:
        inj_s(q)
    vi(v.tensor_copy(T.PF[:, 0:3], T.PI[:, 0:3]))
    vi(v.tensor_scalar(T.PF[:, 5:6], T.PI[:, 0:1], ZS + 0.5, None, OP.is_lt))
    n1 = vi(v.tensor_scalar(T.PF[:, 6:7], T.PI[:, 0:1], ZS + 0.5, None, OP.is_gt))
    for q in V_THEN[:2]:
        inj_v(q)
    need("v", "ldidx", 48)
    need("v", "v", n1)
    n1 = vi(v.tensor_scalar(T.PF[:, 7:8], T.IDX[:, 2:3], T.PF[:, 6:7], T.PF[:, 1:2], OP.mult, OP.add))
    vi(v.tensor_scalar(T.IDY[:, 1:2], T.IDX[:, 1:2], T.PF[:, 1:2], None, OP.add))
    vi(v.tensor_scalar(T.PF[:, 3:4], T.PI[:, 5:6], 4.0, None, OP.mult))
    for q in V_THEN[2:]:
        inj_v(q)
    need("v", "v", n1)
    vID = vi(v.tensor_scalar(T.IDY[:, 0:1], T.IDX[:, 0:1], T.PF[:, 5:6], T.PF[:, 7:8], OP.mult, OP.add))
    need("v", "t", tOFF)
    EARLY = ZS + 15
    vOA = vi(v.tensor_copy(T.OFF[:, 8 * EARLY:256], T.B1[:, 8 * EARLY:256]))
    vOB = vi(v.tensor_copy(T.OFF[:, 0:8 * EARLY], T.B1[:, 0:8 * EARLY]))

    def end(k):
        return T.PW[:, 160 * k + 16:160 * k + 144]

    F = [T.PF[:, c:c + 1] for c in range(8, 16)]
    small = [lambda: s.activation(F[0], T.PI[:, 7:8], FN.Copy, scale=-1.0 / 64),
             lambda: s.activation(F[1], T.PI[:, 7:8], FN.Identity, bias=160.0, scale=-0.5),
             lambda: s.activation(F[2], T.PI[:, 6:7], FN.Abs, bias=F[0], scale=0.25),
             lambda: s.activation(F[3], T.PI[:, 7:8], FN.Identity, bias=T.PF[:, 3:4], scale=0.25),
             lambda: s.activation(F[5], F[2], FN.Identity, bias=F[3], scale=F[1]),
             lambda: s.activation(F[6], F[5], FN.Identity, bias=15.0),
             lambda: s.activation(F[7], T.PI[:, 2:3], FN.Identity, bias=F[6], scale=273.0)]
    si(small.pop(0)())
    need("s", "gq", gPW)
    chain, rows = {BS: 0}, list(S_CHAIN)

    def step_s(j):
        need("s", "v", vOA if j >= EARLY else vOB)
        need("s", "s", chain[j + 1])
        win = T.IOTA[:] if j == BS - 1 else blk128(T.WS, j + 1)
        chain[j] = si(s.activation(blk128(T.WS, j) if j else end(2), win.indirect(T.OFF[:, 8 * j:8 * j + 8]), FN.Copy))

    for j in range(BS - 1, -1, -1):
        step_s(j)
        if rows:
            inj_s(rows.pop(0))
        elif small:
            need("s", "s", chain[j] - 1)
            sY = si(small.pop(0)())
    for q in rows + list(S_LAST):
        inj_s(q)

    def row(j):
        return j + 1 if j < ZS else j - ZS if j < ZS + 16 else (j - 15) % 16

    done = {}

    def step(j):
        first = j in (31, ZS + 15, ZS - 1)
        win = blk128(T.INJ, row(j)) if first else end(0) if j + 1 == BS else blk128(T.W, j + 1)
        o = end(0) if j == BS else end(1) if j == ZS + 16 else blk128(T.W, j)
        need("v", *(inj[row(j)] if first else ("v", done[j + 1])))
        need("v", "v", vOA if j >= EARLY else vOB)
        a = win.indirect(T.OFF[:, 8 * j:8 * j + 8])
        if j in (ZS, ZS + 16):
            done[j] = vi(v.tensor_copy(o, a))
        else:
            need("v", *inj[row(j - 1) if j else "joined"])
            done[j] = vi(v.tensor_tensor(o, a, blk128(T.INJ, row(j - 1)) if j else T.WB[:], OP.add))

    need("v", "gq", gPW)
    for n in range(16 - ZS):
        step(ZS + 15 - n)
        step(31 - n)
    sB = chain[0]
    need("v", "s", sY)
    vTL = vi(v.tensor_copy(T.TL[:, 0::2], T.PF[:, 14:16]))
    gi(g.affine_select(T.SC[:], T.ONES[:], [[0, 128]], OP.is_gt, 1.0 / 128, 0, 0))
    iota(T.MT0[:], [[128, 4], [0, 8]], 128 * 129)
    gIO = iota(T.IO0[:], [[-32, 2], [16, 4]], 64 * rank + 32)
    gC = iota(T.IOR[:], [[2, 4]], 0)
    need("g", "v", vID)
    need("g", "ldem", 32)
    for h in range(2):
        g.indirect_dma_start(T.AE[:, 256 * h:256 * h + 256], None, T.emd[:],
                             IndirectOffsetOnAxis(ap=T.IDY[:, h:h + 1], axis=0), bounds_check=511).then_inc(S.ge, 16)
    def turn(k):
        vi(v.transpose(T.TT[:, 288 * k:288 * k + 128], end(k)))
        return vi(v.transpose(T.TT[:, 288 * k + 128:288 * k + 288], T.PW[:, 160 * k:160 * k + 160]))

    later = [j for n in range(ZS) for j in (ZS - 1 - n, BS - 1 - n)]
    need("v", "v", done[BS])
    n = turn(0)
    if rank and sends:
        need("v", "v", done[ZS + 16])
        n = turn(1)
    step(later.pop(0))
    need("v", "v", max(n, vTL))
    if rank and sends:
        n = vi(v.tensor_copy(T.LS[:, 0:16], T.TT[:, 0:576].indirect(T.TL[:, 2:3])))
        need("g", "v", n)
        send(after(T, rank), "arr%d" % rank, T.LS[:, 0:16], T.LR[:, 24 * rank - 24:24 * rank - 8])
        need("v", "s", sB)
        m = turn(2)
    else:
        n = vi(v.tensor_copy(T.LS[:, 0:16], T.TT[:, 0:288].indirect(T.TL[:, 0:1])))
        step(later.pop(0))
        need("v", "s", sB)
    need("s", "v", max(n, done[ZS + 16]))
    sWA = si(s.activation(T.WA[:], end(1).indirect(T.LS[:, 0:8]), FN.Copy))
    if rank == 0:
        n = vi(v.tensor_copy(T.U[:, 0:2], T.PW[:, 336:338]))
        m = turn(2)
        need("v", "s", sWA)
        need("v", "v", n)
        n = vi(v.tensor_copy(T.U[:, 16:32], T.WA[:].indirect(T.U[:, 0:1])))
        need("g", "v", n)
        send(after(T, rank), "u0", T.U[:, 16:18], T.UR[:, 0:2])
    else:
        if not sends:
            m = turn(2)
        step(later.pop(0))
    need("v", "v", m)
    vL = vi(v.tensor_copy(T.LS[:, 16:32], T.TT[:, 576:864].indirect(T.TL[:, 0:1])))
    if rank and sends:
        need("g", "v", vL)
        send(after(T, rank), "lst%d" % rank, T.LS[:, 16:24], T.LR[:, 24 * rank - 8:24 * rank])
    need("g", "gq", gC)
    n2 = gi(g.affine_select(T.BLKA[:], T.SC[:], [[-16, 8], [0, 16]], OP.is_ge, 0.0, 0, 1))
    gi(g.affine_select(T.MT1[:], T.MT0[:], [[0, 4], [-16, 8]], OP.is_ge, 1e6, 0, 1))
    need("g", "gq", n2)
    n2 = gi(g.affine_select(T.BLK[:], T.BLKA[:], [[16, 8], [0, 16]], OP.is_ge, 0.0, 15, -1))
    iota(T.CN[:], [[0, 2]], -16512)
    need("g", "gq", n2)
    gi(g.affine_select(T.TRI[:], T.BLK[:], [[1, 128]], OP.is_gt, 0.0, 0, -1))
    gi(g.affine_select(T.BH[:], T.BLK[:], [[0, 8], [1, 16]], OP.is_ge, 0.0, -ZS - 1, 0))
    gT = gi(g.affine_select(T.BL[:], T.BLK[:], [[16, 8], [0, 16]], OP.is_ge, 0.0, ZS, -1))
    gi(g.affine_select(T.MT[:], T.MT1[:], [[0, 4], [16, 8]], OP.is_ge, 1e6, 15, -1))
    iota(T.IOTAM[:], [[-32, 2], [1, 35]], -3)
    iota(T.IOTAZ[:], [[1, 100]], -3)
    if not sends:
        gi(g.affine_select(T.ID[:], T.ONES[:], [[1, 128]], OP.is_equal, 0.0, 0, -1))
    if rank == 0:
        iota(T.WP[:, 0:32], [[0, 32]], 0)
    gALL = cnt["gq"]
    need("s", "gq", gIO)
    sIO = si(s.activation(T.IO[:], T.IO0[:], FN.Identity, bias=T.PF[:, 0:1]))
    sDB = si(s.activation(T.DIAGB[:], T.MASKQ[:], FN.Copy, scale=16448.5))
    need("s", "s", sWA)
    need("s", "v", vL)
    sWB = si(s.activation(T.WB[:], T.WA[:].indirect(T.LS[:, 16:24]), FN.Copy, scale=T.PF[:, 6:7]))
    sVZ = si(s.activation(T.VBZ[:, 0:512], T.WS[:, 128:640], FN.Copy, scale=0.0))
    ucol, L, vU = T.UR[:, 0:1], 0, 0
    if rank == 0:
        vU = vi(v.memset(T.UR[:], 0))
    made = {}

    def compose(q, r, k):
        need(q, ("arr%d" if k < 2 else "lst%d") % r, from_parts([r]))
        if k:
            need(q, *made[r, k - 1])
        a = 24 * r - (16, 24, 8)[k]
        o, win = blk128(T.CW, 3 * r - 3 + k), (blk128(T.CW, 3 * r - 4 + k) if k else T.IOTA[:]).indirect(T.LR[:, a:a + 8])
        made[r, k] = (q, vi(v.tensor_copy(o, win)) if q == "v" else si(s.activation(o, win, FN.Copy)))

    inj["joined"] = ("s", sWB)
    fill = [lambda j=j: step(j) for j in later if j != ZS]
    while len(fill) > V_LEFT:
        fill.pop(0)()
    need("v", "gq", gC)
    vRP = vi(v.tensor_scalar(T.REP[:], T.IOR[:], T.PF[:, 2:3], None, OP.add))
    for q, r, k in MAKES:
        if r < rank:
            compose(q, r, k)
        elif q == "v" and fill:
            fill.pop(0)()
    need("t", "gq", gT)
    t.matmul(T.B6[:, 0:2], T.TRI[:], T.CN[:], True, False)
    for col, mat in enumerate((T.BH, T.BL)):
        t.matmul(T.B6[:, col:col + 1], mat[:], T.CN[:, 0:1], False, False)
        t.matmul(T.B4[:, 0:1], T.BLK[:], T.CN[:, 0:1], col == 0, False)
    if rank:
        need("v", "u0", from_parts([0]))
    last = (T.IOTA[:], ucol, 0)
    for r in range(1, rank):
        last = (blk128(T.CW, 3 * r - 1), ucol, max(vU, made[r, 2][1] * (made[r, 2][0] == "v")))
        need("v", "v", vU)
        need("v", *made[r, 2])
        vU = vi(v.tensor_copy(T.U[:, 16 * r:16 * r + 16], last[0].indirect(ucol)))
        ucol = T.U[:, 16 * r:16 * r + 1]
        if fill:
            fill.pop(0)()
    while fill:
        fill.pop(0)()
    need("s", "v", done[ZS + 1])
    sW = si(s.activation(blk128(T.W, ZS), blk128(T.W, ZS + 1).indirect(T.OFF[:, 8 * ZS:8 * ZS + 8]), FN.Copy))
    if rank:
        need("s", "u0", from_parts([0]))
        need("s", "v", last[2])
        need("s", "s", sW - 1)
        sU = si(s.activation(T.UF[:], last[0].indirect(last[1]), FN.Copy, scale=T.MASKQ[:, 0:1]))
        need("v", "s", sU)
    sVZ = si(s.activation(T.VBZ[:, 512:1024], T.WS[:, 128:640], FN.Copy, scale=0.0))
    need("v", "v", max(vU, done[0]))
    a, b = L % 2, ZS % 2
    lists = (T.SA[:, a + L:a + L + 1], T.S0[:, b + ZS:b + ZS + 1])
    n = vi(v.tensor_scalar(T.SA[:, a:a + 16], blk128(T.W, 0).indirect(ucol), T.UF[:, 0:1] if rank else 0.0, None, OP.add))
    need("v", "s", sW)
    need("v", "v", n)
    vS = vi(v.tensor_copy(T.S0[:, b:b + 16], blk128(T.W, ZS).indirect(lists[0])))
    need("v", "s", sDB)
    v.wait_ge(S.ge, 32)
    vC, vE = {}, {}
    for h in range(2):
        need("v", "v", vS if h else 0)
        vE[h] = vi(v.tensor_tensor(T.EM[:, 16 * h:16 * h + 16], blk128(T.AE, 2 * h).indirect(lists[h]), T.MASKQ[:], OP.mult))
        vC[h] = vi(v.tensor_tensor(T.CM[:, 16 * h:16 * h + 16], blk128(T.AE, 2 * h + 1).indirect(lists[h]), T.DIAGB[:], OP.add))
    for h in range(2):
        need("v", "v", vE[h])
        vR = vi(v.tensor_reduce(T.E2[:, h:h + 1], T.EM[:, 16 * h:16 * h + 16], AxisListType.X, OP.max))
        need("v", "v", vC[h])
        vC[h] = vi(v.tensor_reduce(T.CS[:, h:h + 1], T.CM[:, 16 * h:16 * h + 16], AxisListType.X, OP.max))
    for h in range(2):
        need("t", "v", vC[h])
        t.matmul(T.B6[:, h:h + 1], T.TRI[:], T.CS[:, h:h + 1], False, False)
        m = t.matmul(T.B6[:, 1 - h:2 - h], (T.BL, T.BH)[h][:], T.CS[:, h:h + 1], False, h == 1)
    tB = ti(m)
    for h in range(2):
        m = t.matmul(T.B4[:, 0:1], T.BLK[:], T.CS[:, h:h + 1], False, h == 1)
    tN = ti(m)
    need("v", "gq", gALL)
    need("v", "v", vC[0])
    vi(v.tensor_scalar(T.GTB[:, 0:32], T.MT[:], T.CS[:, 0:1], None, OP.is_lt))
    need("v", "v", vR)
    vi(v.tensor_scalar(T.D[:, 0::4], T.E2[:], 63, None, OP.bitwise_and))
    for m in range(1, 4):
        vD = vi(v.tensor_scalar(T.D[:, m::4], T.E2[:], 6 * m, 63, OP.logical_shift_right, OP.bitwise_and))
    need("v", "v", vC[1])
    vG = vi(v.tensor_scalar(T.GTB[:, 32:64], T.MT[:], T.CS[:, 1:2], None, OP.is_lt))
    need("v", "t", tB)
    wide = 67 if sends else 32
    for h in range(2):
        vO = vi(v.tensor_scalar(T.OHM[:, 70 * h:70 * h + 35], T.IOTAM[:, 0:35], T.B6[:, h:h + 1], None, OP.is_equal))
        need("v", "v", vG if h else max(vD, vRP))
        need("v", "s", sVZ)
        vO = vi(v.tensor_tensor(T.VBZ[:, 512 * h:512 * h + 512:16], T.D[:].indirect(T.REP[:, 2 * h:2 * h + 2]),
                                T.GTB[:, 32 * h:32 * h + 32], OP.mult))
        if sends:
            need("v", "t", tN)
            vO = vi(v.tensor_scalar(T.OHM[:, 70 * h + 35:70 * h + 70], T.IOTAM[:, 35:70], T.B4[:, 0:1], T.B6[:, h:h + 1],
                                    OP.add, OP.is_equal))
        if sends and h == 0:
            vN = vi(v.tensor_copy(T.CNT[:], T.B4[:, 0:1]))
            need("g", "v", vN)
            send(after(T, rank)[::-1], "cn", T.CNT[:], T.MR[:, rank:rank + 1], "rest")
        need("t", "v", vO)
        for m in range(4):
            ins = t.matmul(T.B5[:, 0:wide], blk128(T.VBZ, 4 * h + m), T.OHM[:, 70 * h + 3 - m:70 * h + 3 - m + wide],
                           h + m == 0, h + m == 4)
    tM = ti(ins)
    if not sends:
        need("v", "t", tN)
        vN = vi(v.tensor_copy(T.CNT[:], T.B4[:, 0:1]))
    for h in range(2):
        vO = vi(v.tensor_scalar(T.OHZ[:, 100 * h:100 * h + 100], T.IOTAZ[:], T.B6[:, h:h + 1], None, OP.is_equal))
    need("v", "s", sIO)
    need("v", "v", vN)
    if sends:
        vi(v.tensor_scalar(T.GAP[:], T.CNT[:], -1.0, 96.0, OP.mult, OP.add))
        n = vi(v.tensor_scalar(T.IO[:, 4:8], T.IO[:, 4:8], T.CNT[:], None, OP.subtract))
    else:
        n = vO = vi(v.tensor_scalar(T.GE[:], T.IOTA[:, 0:96], T.CNT[:], -1.0, OP.is_ge, OP.mult))
    need("v", "t", tM)
    vM = vi(v.tensor_copy(T.MS[:, 0:wide], T.B5[:, 0:wide]))
    need("g", "gq", gALL)
    need("g", "v", vM)
    g.remote_dma_fused([transfer(to, engines, "z", *((T.MS[:, 35:67], T.WP[:, 0:32]) if to[0] > rank else
                                                     (T.MS[:, 0:32], T.WP[:, 128:160])))
                        for to, engines in deal(topo, T, rank, beside(T, rank), "both")], local_sem=S.lsf)
    g.wait_ge(S.lsf, cnt["lsf"])
    need("t", "v", vO)
    for k in range(8):
        a = 100 * (k // 4) + 3 - k % 4
        ins = t.matmul(T.B7[:, 0:96], blk128(T.VBZ, k), T.OHZ[:, a:a + 96], k == 0, k == 7 and sends)
    if not sends:
        ins = t.matmul(T.B7[:, 0:96], T.ID[:], T.GE[:], False, True)
    tZ = ti(ins)
    need("s", "t", tZ)
    sZ = si(s.activation(T.WP[:, 32:128], T.B7[:, 0:96], FN.Copy))
    if rank:
        need("v", "cn", from_parts(range(rank), after, "rest"))
        n = vi(v.tensor_reduce(T.SUM[:], T.MR[:, 0:rank], AxisListType.X, OP.add))
    need("v", "v", n)
    before = T.SUM[:] if rank else 0.0
    if sends:
        vi(v.tensor_scalar(T.IP[:, 0:4], T.IO[:, 0:4], before, None, OP.subtract))
        n = vi(v.tensor_scalar(T.IP[:, 4:8], T.IO[:, 4:8], before, 0.0, OP.subtract, OP.is_ge))
        need("v", "v", n)
        for c in range(4):
            n = vi(v.tensor_scalar(T.YL[:, c:c + 1], T.IP[:, 4 + c:5 + c], T.GAP[:], T.IP[:, c:c + 1], OP.mult, OP.add))
    else:
        n = vi(v.tensor_scalar(T.YL[:], T.IO[:, 0:4], before, None, OP.subtract))
    need("v", "v", n)
    need("v", "s", sZ)
    need("v", "z", from_parts(beside(T, rank), beside, "both"))
    n = vi(v.tensor_copy(T.YS[:], T.WP[:, 0:160 if sends else 128].indirect(T.YL[:])))
    need("y", "v", n)
    y.dma_start(T.y[:], T.YS[0::16, :]).then_inc(S.st, 16)
    y.wait_ge(S.st, 16)
